import numpy as np, ml_dtypes
CORES = [24,25,26,27,28,29,30,31]
N = 8
import mx_ref
BF = ml_dtypes.bfloat16
def entries(a):
    return np.ascontiguousarray(a.T).reshape(-1)
def table(e):
    return np.ascontiguousarray(np.reshape(e, (-1, 16)).T).astype(np.int32)
def cols(t, e):
    v = np.concatenate([t.reshape(128, -1, 4), np.zeros((128, 1, 4), BF)], axis=1)
    return np.ascontiguousarray(v[:, e]).reshape(128, -1)
def f(rng, *shape):
    return mx_ref.flush((rng.standard_normal(shape, dtype=np.float32) * np.exp2(rng.integers(-2, 3, shape[:-1] + (1,)))).astype(BF))
def wide(rng, *shape, cols=0):
    v = rng.standard_normal(shape, dtype=np.float32) * np.exp2(rng.integers(-12, 13, shape)).astype(np.float32)
    if cols: v *= np.repeat(np.exp2(rng.integers(-cols, cols + 1, shape[:-2] + (1, shape[-1] // 4))) * (rng.random(shape[:-2] + (1, shape[-1] // 4)) > 0.0625), 4, axis=-1).astype(np.float32)
    return mx_ref.flush(v.astype(BF))
T, S, O, CAPP = 256, 512, 2, (128, 192, 256)
B = len(CAPP)
def wanters(q, b):
    return sum(1 << e for e in range(N) if (e ^ q ^ (1 << b)) % (2 << b) == 0)
def holders(q, b):
    return (q >> b) << b, ((q >> b) + 1) << b
def limit(rng, m, keep, lo, hi, s, most):
    v = m.reshape(-1)
    e = np.flatnonzero(v[lo * T:hi * T] & s) + lo * T
    e = e[np.argsort(rng.random(len(e)) - ((keep.reshape(-1)[e] & s) != 0))][most:]
    v[e] &= ~s
def masks(rng, keep=None, off=None, share=0.55):
    keep = np.zeros((N, T), int) if keep is None else keep
    off = np.zeros((N, T), bool) if off is None else off
    for r in range(N):
        if not ((keep >> r) & 1).any(): keep[r, rng.choice(np.flatnonzero(~off[r]))] |= 1 << r
    n = rng.integers(1, 4, (N, T)) * (rng.random((N, T)) < share)
    m = ((np.argsort(rng.random((N, T, N)), axis=2) < n[:, :, None]) * (1 << np.arange(N))).sum(axis=2)
    m = np.ascontiguousarray(np.where(off, 0, m) | keep)
    for b in range(B):
        for q in range(N): limit(rng, m, keep, *holders(q, b), wanters(q, b), CAPP[b])
    for r in range(N): limit(rng, m, keep, 0, N, 1 << r, S)
    return {"dm": np.stack([table(v) for v in m])}
def setup_inputs(rng):
    return {"x": f(rng, N, 128, 4 * T), **masks(rng), "w": f(rng, N, 128, 512 * O)}
def setup_inputs_comb(rng):
    k = np.zeros((N, T), int); c = np.arange(T); s = int(rng.integers(0, 16)); p = int(rng.integers(0, N)); g = p ^ (N >> 1)
    for e in range(N): k[:, (c - e - s) % 4 == 0] |= 1 << e
    lo, hi = holders(p, B - 1)
    k[lo:hi] &= ~(1 << g)
    k[p, c % 16 != s] |= 1 << g
    assert not check_inputs({"dm": np.stack([table(v) for v in k])})
    return {**setup_inputs(rng), **masks(rng, k)}
def setup_inputs_turn(rng):
    k = np.zeros((N, T), int); g = int(rng.integers(0, N))
    k[g ^ 1, rng.permutation(T)[:CAPP[0]]] |= 1 << g
    k[g ^ 3, rng.permutation(T)[:CAPP[0]]] |= 1 << g
    h = rng.permutation(T)
    k[g, h[:CAPP[0]]] |= 1 << (g ^ 3)
    k[g, h[CAPP[0]:2 * CAPP[0]]] |= 1 << (g ^ 2)
    if N == 8: k[g ^ 6, rng.permutation(T)[:CAPP[1]]] |= 1 << (g ^ 4)
    return {**setup_inputs(rng), **masks(rng, k)}
def setup_inputs_none(rng):
    z = np.zeros((N, T), bool); k = np.zeros((N, T), int); p = int(rng.integers(0, N))
    for r in range(N): z[r, rng.permutation(T)[:T // 2]] = True
    k[p ^ 1, rng.choice(np.flatnonzero(~z[p ^ 1]))] |= 1 << p
    d = {**setup_inputs(rng), **masks(rng, k, off=z, share=1)}
    d["dm"][p] = 0
    return d
def setup_inputs_full(rng):
    k = np.zeros((N, T), int); g = int(rng.integers(0, N)); s = int(rng.integers(0, T))
    k[g ^ 1, (np.arange(CAPP[0]) + s) % T] |= 1 << (g ^ 2)
    k[g, (np.arange(S - sum(CAPP[1:])) + s) % T] |= 1 << g
    for b in range(1, B):
        for r in range(N):
            if r >> b == (g >> b) ^ 1: k[r, (np.arange(CAPP[b] >> b) + s) % T] |= 1 << g
    assert not check_inputs({"dm": np.stack([table(v) for v in k])})
    return {**setup_inputs(rng), **masks(rng, k, share=1)}
def setup_inputs_spread(rng):
    d = setup_inputs(rng); d["x"] = wide(rng, N, 128, 4 * T, cols=8); return d
def check_inputs(d):
    bad = []
    m = np.stack([entries(v) for v in d["dm"]]).astype(np.int64)
    if m.min() < 0 or m.max() >= 1 << N: bad.append("dm")
    for r in range(N):
        if ((m >> r) & 1).sum() > S: bad.append("arrivals")
    for b in range(B):
        for q in range(N):
            lo, hi = holders(q, b)
            if ((m[lo:hi] & wanters(q, b)) != 0).sum() > CAPP[b]: bad.append("CAPP_" + str(b))
    return bad
def reference(x, dm, w):
    m = np.stack([entries(v) for v in dm])
    every = np.concatenate(list(x), axis=1)
    y = np.zeros((N, 128, O * S), np.float32); ln = np.zeros((N, 1, 2), np.float32)
    for r in range(N):
        e = np.flatnonzero((m.reshape(-1) >> r) & 1); n = len(e)
        k = np.full(S, -1); k[:n] = e
        a = mx_ref.quantize(cols(every, k))
        for o in range(O):
            y[r][:, S * o:S * o + n] = mx_ref.matmul(mx_ref.quantize(np.ascontiguousarray(w[r][:, 512 * o:512 * o + 512])), a)[:, :n]
        ln[r, 0, 0] = n; ln[r, 0, 1] = np.count_nonzero((m[r] >> r) & 1)
    return {"y": y, "ln": ln}

@@ -1,0 +1,379 @@
+from concourse.bass import DstId, RemoteDMATransfer
+from concourse.mybir import dt, AluOpType, AxisListType, ActivationFunctionType
+
+F32, I32, BF, U16, U8, Q8 = "float32", "int32", "bfloat16", "uint16", "uint8", "float8_e4m3fn_x4"
+LB = 1024
+CAP = (128, 192, 256)
+
+
+def _s(n, d):
+    return ("sbuf", [128, n], d)
+
+
+SCRATCH = {
+    "dmx": _s(64, I32), "xt": _s(1024, BF), "wt": _s(1024, BF), "zt": _s(512, BF),
+    "q0": _s(384, Q8), "s0": _s(384, U8), "q1": _s(512, Q8), "s1": _s(512, U8),
+    "q2": _s(704, Q8), "s2": _s(704, U8), "q3": _s(512, Q8), "s3": _s(512, U8),
+    "slq0": _s(128, Q8), "sls0": _s(128, U8), "slq1": _s(192, Q8), "sls1": _s(192, U8),
+    "slq2": _s(256, Q8), "sls2": _s(256, U8),
+    "qa": _s(512, Q8), "sa": _s(512, U8), "qb": _s(512, Q8), "sb8": _s(512, U8), "wq": _s(256, Q8), "ws": _s(256, U8),
+    "pid": _s(1, I32), "pi": _s(4, I32), "pf": _s(4, F32), "r32": _s(4, F32), "ir": _s(64, F32), "tri": _s(64, F32),
+    "fj": _s(64, F32), "cf": _s(64, F32), "vraw": _s(128, F32), "v1r": _s(256, F32), "dupf": _s(4, F32), "dup": _s(4, U16),
+    "ramp": _s(576, F32), "res": _s(104, F32), "i128f": _s(32, F32), "i128": _s(32, F32), "c8": _s(8, F32),
+    "and0": _s(8, I32), "sel0": _s(8, F32), "inc0": _s(8, F32), "x0": _s(32, F32), "x0t": _s(32, F32), "b0": _s(1, F32),
+    "ya0": _s(8, F32), "yb0": _s(8, F32), "yc0": _s(8, F32), "p0": _s(8, U16),
+    "and1": _s(104, I32), "sel": _s(136, F32), "inc1": _s(40, F32), "x1": _s(96, F32), "x1t": _s(96, F32), "b1": _s(4, F32),
+    "ya1": _s(16, F32), "yb1": _s(16, F32), "yc1": _s(16, F32), "p0k": _s(8, U16), "p1": _s(16, U16),
+    "tt": _s(96, F32), "st": _s(32, U16), "vr2": _s(512, F32), "inc2": _s(64, F32), "x2": _s(128, F32), "x2t": _s(128, F32),
+    "b2": _s(1, F32), "n2o": _s(1, F32), "b3": _s(1, F32), "nh": _s(1, F32), "n2": _s(1, F32),
+    "ya2": _s(64, F32), "yb2": _s(64, F32), "yc2": _s(64, F32), "p2": _s(32, U16), "p3": _s(32, U16),
+    "win0": _s(LB + 128, F32), "win1": _s(LB + 192, F32), "win2": _s(LB + 256, F32), "win3": _s(LB + 512, F32),
+    "tr0": _s(128, F32), "tr1": _s(192, F32), "tr2": _s(256, F32), "tr3": _s(512, F32), "al": _s(128, F32),
+    "ta": _s(128, F32), "tb": _s(256, F32), "tc": _s(256, F32),
+    "off0": _s(8, U16), "off1": _s(12, U16), "off2": _s(16, U16), "off3": _s(32, U16), "offbf": _s(32, F32), "offb": _s(32, U16),
+    "lnt": _s(4, F32), "ys": _s(1024, F32),
+    "ps": ("psum", [128, 2048], F32),
+}
+SEMAPHORES = ["ld", "lx", "lw", "v", "s", "t", "gp", "mk", "r0c", "r0s", "r1c", "r1s", "r2c", "r2s", "rn",
+              "cp", "cr", "lo", "yo", "lnd"]
+
+
+def wanters(q, b):
+    return sum(1 << e for e in range(8) if (e ^ q ^ (1 << b)) % (2 << b) == 0)
+
+
+def rank_program(g, core, T, topo):
+    q = T.rank_of(core)
+    if q is None:
+        return
+    A, X, CP = AluOpType, AxisListType.X, ActivationFunctionType.Copy
+    S = T.sem
+    p4, half = q & 3, q >> 2
+    own = slice(16 * p4, 16 * p4 + 15)
+    queues = {"v": g.vector, "s": g.scalar, "t": g.tensor, "gp": g, "y": g.sync}
+    n, seen = {"v": 0, "s": 0, "t": 0, "gp": 0}, {}
+
+    def need(queue, sem, count):
+        if seen.get((queue, sem), 0) < count:
+            queues[queue].wait_ge(S[sem], int(count))
+            seen[(queue, sem)] = count
+
+    def done(kind, ins):
+        ins.then_inc(S[kind], 1)
+        n[kind] += 1
+        return n[kind]
+
+    def V(ins):
+        return done("v", ins)
+
+    def vv(count=None):
+        need("v", "v", n["v"] if count is None else count)
+
+    ts, tt_, cp = g.vector.tensor_scalar, g.vector.tensor_tensor, g.vector.tensor_copy
+    red, tp, scan = g.vector.tensor_reduce, g.vector.transpose, g.vector.tensor_tensor_scan
+
+    def to(d):
+        return T.cores[d]
+
+    def send(dst, out, in_, sem):
+        rid, pid, _ = topo.addr(to(dst))
+        g.remote_dma(out, in_, S[sem], S.lo, pid, rid, topo.mask(core, to(dst)))
+
+    for a in range(4):
+        for h in range(2):
+            e = g.sync if h == 0 else g.scalar
+            e.dma_start(T.dmx[32 * a + 16 * h:32 * a + 16 * h + 16, own], T.dm[:, h:h + 15]).then_inc(S.ld, 16)
+    g.sync.dma_start(T.xt[:], T.x[:]).then_inc(S.lx, 16)
+    g.scalar.dma_start(T.wt[:], T.w[:]).then_inc(S.lw, 16)
+
+    def iota(out, pat, base, cm):
+        return done("gp", g.iota(out, pat, base, cm, allow_small_or_imprecise_dtypes=True))
+
+    k_pid = done("gp", g.iota(T.pid[:], [[0, 1]], 0, 1))
+    k_ir = iota(T.ir[:], [[0, 2], [1, 32]], 0, 0)
+    k_dup = iota(T.dupf[:], [[16, 2], [0, 2]], 0, 0)
+    k_c8 = iota(T.c8[:], [[32, 8]], 0, 0)
+    k_vraw = iota(T.vraw[:], [[32, 8], [1, 16]], 128, 0)
+
+    k_zt = V(g.vector.memset(T.zt[:], 0.0))
+    k_res = V(g.vector.memset(T.res[:], 1.0))
+    V(g.vector.memset(T.tri[:, 32:64], 1.0))
+    k_w0 = V(g.vector.memset(T.win0[:, LB:LB + 128], 128.0))
+    vv(k_res)
+    V(g.vector.memset(T.res[:, 8:40:16], 0.0))
+    V(g.vector.memset(T.res[:, 72:73], 0.0))
+    need("v", "gp", k_pid)
+    for j, m in enumerate((31, 15, 16)):
+        k = V(ts(T.pi[:, j:j + 1], T.pid[:], m, None, A.bitwise_and))
+    vv(k)
+    k = V(cp(T.pf[:, 0:3], T.pi[:, 0:3]))
+    vv(k)
+    k = V(ts(T.r32[:, 0:1], T.pf[:, 1:2], 32.0, None, A.mult))
+    need("v", "gp", k_ir)
+    V(ts(T.tri[:, 0:32], T.ir[:, 0:32], T.pf[:, 0:1], None, A.is_gt))
+    vv(k)
+    V(ts(T.fj[:], T.ir[:], T.r32[:, 0:1], None, A.add))
+    V(ts(T.cf[:], T.ir[:], T.r32[:, 0:1], float(1 - LB), A.add, A.add))
+    need("v", "gp", k_dup)
+    V(ts(T.dup[:], T.dupf[:], T.pf[:, 1:2], None, A.add))
+    need("v", "gp", k_vraw)
+    o1, o2 = 128 * (q & 1), 128 * (1 - (q & 1))
+    V(ts(T.v1r[:, o1:o1 + 128], T.vraw[:], T.pf[:, 2:3], None, A.add))
+    V(ts(T.sel[:, 104 + 8 * p4:112 + 8 * p4], T.c8[:], T.pf[:, 0:1], None, A.add))
+    V(g.vector.memset(T.al[:], 0.0))
+    V(g.vector.memset(T.win1[:, LB:LB + 192], 128.0))
+    V(g.vector.quantize_mx(T.q2[:, 0:128], T.s2[:, 0:128], T.zt[:]))
+    need("s", "v", k_zt)
+    done("s", g.scalar.activation(T.win2[:, LB:LB + 256], T.zt[:, 0:256], CP))
+    k_fill = done("s", g.scalar.activation(T.win3[:, LB:LB + 512], T.zt[:], CP))
+
+    peers = [q ^ 1, q ^ 2, q ^ 3]
+    g.wait_ge(S.ld, 128)
+    m = topo.mask(core, to(peers[0]))
+    for d in peers:
+        m &= topo.mask(core, to(d))
+    ids = []
+    for d in peers:
+        rid, pid, _ = topo.addr(to(d))
+        ids.append(DstId(rid=rid, pnc=pid))
+    g.remote_dma_fused([RemoteDMATransfer(dst_ids=ids, dma_engine_mask=m, remote_sem=S.mk, srcs=[T.dmx[:, own]],
+                                          dsts=[T.dmx[:, own] for d in peers])], local_sem=S.lo)
+    n_lo = 16
+    iota(T.ramp[:, 256:384], [[16, 4], [64, 2], [1, 16]], 384, 0)
+    iota(T.ramp[:, 0:256], [[1, 256]], 128, 0)
+    k_ramp = iota(T.ramp[:, 384:576], [[1, 192]], 512, 0)
+    if half == 0:
+        k_i128 = iota(T.i128f[:], [[16, 32]], 128, 0)
+
+    def table(i, count, off, plain=False):
+        win, tr, nb = T["win%d" % i], T["tr%d" % i], count // 32
+        vv()
+        k = V(tp(tr[:, 0:count], win[:, LB:LB + count]))
+        vv(k)
+        al = T.al[:, 32 * i:32 * i + 32]
+        dst = T.al[:, 32 * i:32 * i + 32:8] if plain else T.al[:, 32 * i:32 * i + nb]
+        k = V(tt_(dst, tr[:, 0:count:32], tr[:, 16:count:32], A.max))
+        vv(k)
+        k = V(tp(T.ta[:, 32 * i:32 * i + 32], al))
+        vv(k)
+        k = V(cp(T.tb[:, 64 * i:64 * i + 64], T.ta[:, 32 * i:32 * i + 32].indirect(T.dup[:])))
+        vv(k)
+        k = V(tp(T.tc[:, 64 * i:64 * i + 64], T.tb[:, 64 * i:64 * i + 64]))
+        vv(k)
+        if plain:
+            k = V(cp(off[:], T.tc[:, 64 * i:64 * i + 64:8]))
+        else:
+            V(cp(off[:, 0:2 * nb:2], T.tc[:, 64 * i:64 * i + nb]))
+            k = V(cp(off[:, 1:2 * nb:2], T.tc[:, 64 * i + 32:64 * i + 32 + nb]))
+        return k
+
+    def pick(qo, so, qi, si, off, k_off, vwaits=(), swaits=()):
+        vv(k_off)
+        for w in vwaits:
+            need("v", *w)
+        a = V(cp(qo.bitcast(dt.uint32), qi.bitcast(dt.uint32).indirect(off)))
+        need("s", "v", k_off)
+        for w in swaits:
+            need("s", *w)
+        return a, done("s", g.scalar.activation(so, si.indirect(off), CP))
+
+    need("v", "ld", 128)
+    k = V(ts(T.and0[:], T.dmx[:, 16 * p4:16 * p4 + 15:2], wanters(q, 0), None, A.bitwise_and))
+    vv(k)
+    k = V(ts(T.sel0[:], T.and0[:], 0.0, None, A.is_gt))
+    vv(k)
+    k = V(scan(T.inc0[:], T.res[:, 0:8], T.sel0[:], 0.0, A.mult, A.add))
+    vv(k)
+    k = V(ts(T.x0[:], T.tri[:, 0:32], T.inc0[:, 7:8], None, A.mult))
+    ka = V(tt_(T.ya0[:], T.inc0[:], T.cf[:, 0:8], A.subtract))
+    vv(k)
+    k = V(tp(T.x0t[:], T.x0[:]))
+    vv(ka)
+    ka = V(tt_(T.yb0[:], T.ya0[:], T.sel0[:], A.mult))
+    vv(k)
+    k = V(red(T.b0[:], T.x0t[:], X, A.add))
+    vv(ka)
+    ka = V(tt_(T.yc0[:], T.yb0[:], T.fj[:, 0:8], A.add))
+    vv(ka)
+    k = V(ts(T.p0[:], T.yc0[:], T.b0[:], None, A.add))
+    vv(k)
+    V(cp(T.win0[:].indirect(T.p0[:]), T.v1r[:, o1:o1 + 128]))
+    need("v", "lx", 16)
+    k_q = V(g.vector.quantize_mx(T.q0[:, 128:384], T.s0[:, 128:384], T.xt[:]))
+    k_off = table(0, 128, T.off0, plain=True)
+    ka, ks = pick(T.slq0[:], T.sls0[:], T.q0[:], T.s0[:], T.off0[:], k_off)
+    need("y", "v", k_q)
+    for dq, ds in ((T.q1, T.s1), (T.q2, T.s2)):
+        g.sync.dma_start(dq[:, 128:384].bitcast(dt.uint8), T.q0[:, 128:384].bitcast(dt.uint8)).then_inc(S.cp, 16)
+        g.sync.dma_start(ds[:, 128:384], T.s0[:, 128:384]).then_inc(S.cp, 16)
+    need("gp", "v", ka)
+    send(q ^ 1, T.q1[:, 384:512].bitcast(dt.uint8), T.slq0[:].bitcast(dt.uint8), "r0c")
+    need("gp", "s", ks)
+    send(q ^ 1, T.s1[:, 384:512], T.sls0[:], "r0s")
+    n_lo += 32
+    need("y", "r0c", 16)
+    g.sync.dma_start(T.q2[:, 384:512].bitcast(dt.uint8), T.q1[:, 384:512].bitcast(dt.uint8)).then_inc(S.cr, 16)
+    need("y", "r0s", 16)
+    g.sync.dma_start(T.s2[:, 384:512], T.s1[:, 384:512]).then_inc(S.cr, 16)
+
+    pa, pb, o = 2 * (p4 >> 1), 2 * (1 - (p4 >> 1)), p4 ^ 1
+    need("v", "mk", 48)
+    V(ts(T.and1[:, 0:8], T.dmx[:, 16 * o:16 * o + 15:2], wanters(q ^ 1, 0), None, A.bitwise_and))
+    V(ts(T.and1[:, 8:24], T.dmx[:, 16 * pa:16 * pa + 31:2], wanters(q, 1), None, A.bitwise_and))
+    k = V(ts(T.and1[:, 24:40], T.dmx[:, 16 * pb:16 * pb + 31:2], wanters(q ^ 2, 1), None, A.bitwise_and))
+    vv(k)
+    k = V(ts(T.sel[:, 0:40], T.and1[:, 0:40], 0.0, None, A.is_gt))
+    vv(k)
+    k = V(scan(T.inc1[:], T.res[:, 0:40], T.sel[:, 0:40], 0.0, A.mult, A.add))
+    vv(k)
+    for j, c in enumerate((7, 23, 39)):
+        k = V(ts(T.x1[:, 32 * j:32 * j + 32], T.tri[:, 0:32], T.inc1[:, c:c + 1], None, A.mult))
+    ka = V(tt_(T.ya1[:], T.inc1[:, 8:24], T.cf[:, 0:16], A.subtract))
+    vv(k)
+    k = V(tp(T.x1t[:], T.x1[:]))
+    vv(ka)
+    ka = V(tt_(T.yb1[:], T.ya1[:], T.sel[:, 8:24], A.mult))
+    vv(k)
+    k0 = V(red(T.b1[:, 0:1], T.x1t[:, 0:32], X, A.add))
+    V(red(T.b1[:, 1:2], T.x1t[:, 32:64], X, A.add))
+    vv(k0)
+    k0 = V(ts(T.p0k[:], T.inc1[:, 0:8], T.b1[:, 0:1], 255.0, A.add, A.add))
+    need("s", "v", k0)
+    need("s", "gp", k_ramp)
+    ks = done("s", g.scalar.activation(T.v1r[:, o2:o2 + 128], T.ramp[:].indirect(T.p0k[:]), CP))
+    k2 = V(red(T.b1[:, 2:3], T.x1t[:, 64:96], X, A.add))
+    ka = V(tt_(T.yc1[:], T.yb1[:], T.fj[:, 0:16], A.add))
+    V(ts(T.sel[:, 104 + 8 * o:112 + 8 * o], T.inc1[:, 0:8], T.b1[:, 0:1], 255.0, A.add, A.add))
+    vv(ka)
+    k = V(ts(T.p1[:], T.yc1[:], T.b1[:, 1:2], None, A.add))
+    V(ts(T.sel[:, 104 + 8 * pb:120 + 8 * pb], T.inc1[:, 24:40], T.b1[:, 2:3], 383.0, A.add, A.add))
+    vv(k)
+    need("v", "s", ks)
+    V(cp(T.win1[:].indirect(T.p1[:]), T.v1r[:]))
+    k_off1 = table(1, 192, T.off1)
+    V(ts(T.and1[:, 40:72], T.dmx[:, 0:63:2], 1 << (q ^ 4), None, A.bitwise_and))
+    k = V(ts(T.and1[:, 72:104], T.dmx[:, 0:63:2], 1 << q, None, A.bitwise_and))
+    vv(k)
+    k = V(ts(T.sel[:, 40:104], T.and1[:, 40:104], 0.0, None, A.is_gt))
+    vv(k)
+    k_tt = V(tp(T.tt[:], T.sel[:, 40:136]))
+    vv(k_tt)
+    k_st = V(cp(T.st[:], T.tt[:, 64:96]))
+    ka, ks = pick(T.slq1[:], T.sls1[:], T.q1[:], T.s1[:], T.off1[:], k_off1,
+                  (("cp", 64), ("r0c", 16)), (("cp", 64), ("r0s", 16)))
+    need("gp", "v", ka)
+    send(q ^ 2, T.q2[:, 512:704].bitcast(dt.uint8), T.slq1[:].bitcast(dt.uint8), "r1c")
+    need("gp", "s", ks)
+    send(q ^ 2, T.s2[:, 512:704], T.sls1[:], "r1s")
+    n_lo += 32
+
+    need("s", "v", k_st)
+    k_vr = done("s", g.scalar.activation(T.vr2[:], T.ramp[:].indirect(T.st[:]), CP))
+    k = V(scan(T.inc2[:], T.res[:, 40:104], T.tt[:, 0:64], 0.0, A.mult, A.add))
+    vv(k)
+    V(ts(T.x2[:, 0:64], T.tri[:], T.inc2[:, 31:32], None, A.mult))
+    k = V(ts(T.x2[:, 64:128], T.tri[:], T.inc2[:, 63:64], None, A.mult))
+    ka = V(tt_(T.ya2[:], T.inc2[:], T.cf[:], A.subtract))
+    vv(k)
+    k = V(tp(T.x2t[:], T.x2[:]))
+    vv(ka)
+    ka = V(tt_(T.yb2[:], T.ya2[:], T.tt[:, 0:64], A.mult))
+    vv(k)
+    k_n2 = V(red(T.n2o[:], T.x2t[:, 32:64], X, A.add))
+    need("gp", "v", k_n2)
+    send(q ^ 4, T.n2[:], T.n2o[:], "rn")
+    n_lo += 16
+    V(red(T.b2[:], T.x2t[:, 0:32], X, A.add))
+    vv(ka)
+    k = V(tt_(T.yc2[:], T.yb2[:], T.fj[:], A.add))
+    vv(k)
+    k = V(ts(T.p2[:], T.yc2[:, 0:32], T.b2[:], None, A.add))
+    vv(k)
+    need("v", "s", k_vr)
+    V(cp(T.win2[:].indirect(T.p2[:]), T.vr2[:]))
+    k_off2 = table(2, 256, T.off2)
+    ka, ks = pick(T.slq2[:], T.sls2[:], T.q2[:], T.s2[:], T.off2[:], k_off2,
+                  (("cp", 64), ("cr", 32), ("r1c", 16)), (("cp", 64), ("cr", 32), ("r1s", 16)))
+    need("gp", "v", ka)
+    send(q ^ 4, T.q3[:, 128:384].bitcast(dt.uint8), T.slq2[:].bitcast(dt.uint8), "r2c")
+    need("gp", "s", ks)
+    send(q ^ 4, T.s3[:, 128:384], T.sls2[:], "r2s")
+    n_lo += 32
+    V(red(T.b3[:], T.x2t[:, 64:96], X, A.add))
+    k = V(red(T.nh[:], T.x2t[:, 96:128], X, A.add))
+    if half == 0:
+        vv(k)
+        k = V(ts(T.p3[:], T.yc2[:, 32:64], T.b3[:], None, A.add))
+    else:
+        vv(k)
+        need("v", "rn", 16)
+        k = V(ts(T.p3[:], T.yc2[:, 32:64], T.b3[:], T.n2[:], A.add, A.add))
+    vv(k)
+    V(cp(T.win3[:].indirect(T.p3[:]), T.vr2[:]))
+    need("v", "lw", 16)
+    k_wq = V(g.vector.quantize_mx(T.wq[:], T.ws[:], T.wt[:]))
+    k_off3 = table(3, 512, T.off3)
+    ka, ks = pick(T.qa[:], T.sa[:], T.q2[:], T.s2[:], T.off3[:], k_off3)
+
+    def mm(qx, sx, c, start, stop):
+        for w in range(2):
+            b = 512 * (2 * w + c)
+            done("t", g.tensor.matmul_mx(T.ps[:, b:b + 256], T.wq[:, 128 * w:128 * w + 128], T.ws[:, 128 * w:128 * w + 128],
+                                         qx, sx, start, stop))
+        return n["t"]
+
+    def store(c, k):
+        need("v", "t", k)
+        need("s", "t", k)
+        a = V(cp(T.ys[:, 256 * c:256 * c + 256], T.ps[:, 512 * c:512 * c + 256]))
+        b = done("s", g.scalar.activation(T.ys[:, 512 + 256 * c:768 + 256 * c], T.ps[:, 1024 + 512 * c:1280 + 512 * c], CP))
+        need("y", "v", a)
+        g.sync.dma_start(T.y[:, 256 * c:256 * c + 256], T.ys[:, 256 * c:256 * c + 256]).then_inc(S.yo, 16)
+        need("y", "s", b)
+        g.sync.dma_start(T.y[:, 512 + 256 * c:768 + 256 * c], T.ys[:, 512 + 256 * c:768 + 256 * c]).then_inc(S.yo, 16)
+
+    need("t", "v", max(ka, k_wq))
+    need("t", "s", ks)
+    k0 = mm(T.qa[:, 0:256], T.sa[:, 0:256], 0, True, False)
+    k1 = mm(T.qa[:, 256:512], T.sa[:, 256:512], 1, True, half == 1)
+    if half == 0:
+        need("v", "gp", k_i128)
+        k = V(ts(T.i128[:], T.i128f[:], T.pf[:, 1:2], None, A.add))
+        vv(k)
+        k = V(ts(T.offbf[:], T.i128[:], T.nh[:], 0.0, A.subtract, A.max))
+        vv(k)
+        k_offb = V(ts(T.offb[:], T.offbf[:], 384.0, None, A.min))
+        V(g.vector.quantize_mx(T.q3[:, 0:128], T.s3[:, 0:128], T.zt[:]))
+        k_z = V(g.vector.quantize_mx(T.q3[:, 384:512], T.s3[:, 384:512], T.zt[:]))
+    else:
+        store(1, k1)
+    need("v", "rn", 16)
+    k = V(tt_(T.lnt[:, 0:1], T.nh[:], T.n2[:], A.add))
+    k = V(red(T.lnt[:, 1:2], T.x2t[:, 96 + 8 * p4:104 + 8 * p4], X, A.add))
+    need("y", "v", k)
+    g.sync.dma_start(T.ln[:], T.lnt[0:1, 0:2]).then_inc(S.lnd, 16)
+
+    if half == 0:
+        need("s", "v", k_z)
+        vv(k_z)
+        ks = []
+        for c in range(2):
+            a, b = 256 * c, 256 * c + 256
+            ka, kb = pick(T.qb[:, a:b], T.sb8[:, a:b], T.q3[:], T.s3[:], T.offb[:, 16 * c:16 * c + 16], k_offb,
+                          (("r2c", 16),), (("r2s", 16),))
+            need("t", "v", ka)
+            need("t", "s", kb)
+            ks.append(mm(T.qb[:, a:b], T.sb8[:, a:b], c, False, True))
+        store(0, ks[0])
+        store(1, ks[1])
+    else:
+        need("t", "r2c", 16)
+        need("t", "r2s", 16)
+        store(0, mm(T.q3[:, 128:384], T.s3[:, 128:384], 0, False, True))
+
+    for kind in ("v", "s", "t"):
+        need("gp", kind, n[kind])
+    g.wait_ge(S.gp, n["gp"])
+    g.wait_ge(S.lo, n_lo)
+    g.wait_ge(S.yo, 64)
+    g.wait_ge(S.lnd, 16)

@@ -3,7 +3,6 @@ from concourse.mybir import dt, AluOpType, AxisListType, ActivationFunctionType
 
 F32, I32, BF, U16, U8, Q8 = "float32", "int32", "bfloat16", "uint16", "uint8", "float8_e4m3fn_x4"
 LB = 1024
-CAP = (128, 192, 256)
 
 
 def _s(n, d):
@@ -13,29 +12,29 @@ def _s(n, d):
 SCRATCH = {
     "dmx": _s(64, I32), "xt": _s(1024, BF), "wt": _s(1024, BF), "zt": _s(512, BF),
     "q0": _s(384, Q8), "s0": _s(384, U8), "q1": _s(512, Q8), "s1": _s(512, U8),
-    "q2": _s(704, Q8), "s2": _s(704, U8), "q3": _s(512, Q8), "s3": _s(512, U8),
+    "q2": _s(704, Q8), "s2": _s(704, U8), "q3": _s(960, Q8), "s3": _s(960, U8),
     "slq0": _s(128, Q8), "sls0": _s(128, U8), "slq1": _s(192, Q8), "sls1": _s(192, U8),
     "slq2": _s(256, Q8), "sls2": _s(256, U8),
-    "qa": _s(512, Q8), "sa": _s(512, U8), "qb": _s(512, Q8), "sb8": _s(512, U8), "wq": _s(256, Q8), "ws": _s(256, U8),
-    "pid": _s(1, I32), "pi": _s(4, I32), "pf": _s(4, F32), "r32": _s(4, F32), "ir": _s(64, F32), "tri": _s(64, F32),
-    "fj": _s(64, F32), "cf": _s(64, F32), "vraw": _s(128, F32), "v1r": _s(256, F32), "dupf": _s(4, F32), "dup": _s(4, U16),
-    "ramp": _s(576, F32), "res": _s(104, F32), "i128f": _s(32, F32), "i128": _s(32, F32), "c8": _s(8, F32),
-    "and0": _s(8, I32), "sel0": _s(8, F32), "inc0": _s(8, F32), "x0": _s(32, F32), "x0t": _s(32, F32), "b0": _s(1, F32),
-    "ya0": _s(8, F32), "yb0": _s(8, F32), "yc0": _s(8, F32), "p0": _s(8, U16),
-    "and1": _s(104, I32), "sel": _s(136, F32), "inc1": _s(40, F32), "x1": _s(96, F32), "x1t": _s(96, F32), "b1": _s(4, F32),
-    "ya1": _s(16, F32), "yb1": _s(16, F32), "yc1": _s(16, F32), "p0k": _s(8, U16), "p1": _s(16, U16),
-    "tt": _s(96, F32), "st": _s(32, U16), "vr2": _s(512, F32), "inc2": _s(64, F32), "x2": _s(128, F32), "x2t": _s(128, F32),
-    "b2": _s(1, F32), "n2o": _s(1, F32), "b3": _s(1, F32), "nh": _s(1, F32), "n2": _s(1, F32),
-    "ya2": _s(64, F32), "yb2": _s(64, F32), "yc2": _s(64, F32), "p2": _s(32, U16), "p3": _s(32, U16),
+    "qa": _s(512, Q8), "sa": _s(512, U8), "wq": _s(256, Q8), "ws": _s(256, U8),
+    "pid": _s(1, I32), "pi": _s(4, I32), "pf": _s(4, F32), "r32": _s(4, F32), "ir": _s(64, F32), "ones": _s(32, F32),
+    "fj": _s(64, F32), "vraw": _s(128, F32), "v1r": _s(256, F32), "dupf": _s(4, F32), "dup": _s(4, U16),
+    "ramp": _s(577, F32), "res": _s(104, F32), "uif": _s(64, F32), "ui": _s(64, F32), "ub": _s(64, F32), "c8": _s(8, F32),
+    "zz": _s(192, F32), "and0": _s(8, I32), "sel0": _s(8, F32), "lf0": _s(8, F32), "x0t": _s(32, F32), "bs0": _s(32, F32),
+    "ya0": _s(8, F32), "yc0": _s(8, F32), "p0": _s(8, U16),
+    "and1": _s(104, I32), "sel": _s(136, F32), "lf1": _s(16, F32), "x1t": _s(32, F32), "bs1": _s(32, F32),
+    "ya1": _s(16, F32), "yc1": _s(16, F32), "p0k": _s(8, U16), "p1": _s(16, U16), "p1r": _s(16, U16),
+    "tt": _s(96, F32), "st": _s(32, U16), "vr2": _s(512, F32), "lf2": _s(64, F32), "inc2": _s(64, F32), "x2t": _s(64, F32),
+    "bs2": _s(64, F32), "tn": _s(64, F32), "tnt": _s(64, F32), "n2": _s(1, F32),
+    "ya2": _s(64, F32), "yc2": _s(64, F32), "p2": _s(32, U16), "p3": _s(32, U16),
     "win0": _s(LB + 128, F32), "win1": _s(LB + 192, F32), "win2": _s(LB + 256, F32), "win3": _s(LB + 512, F32),
     "tr0": _s(128, F32), "tr1": _s(192, F32), "tr2": _s(256, F32), "tr3": _s(512, F32), "al": _s(128, F32),
-    "ta": _s(128, F32), "tb": _s(256, F32), "tc": _s(256, F32),
-    "off0": _s(8, U16), "off1": _s(12, U16), "off2": _s(16, U16), "off3": _s(32, U16), "offbf": _s(32, F32), "offb": _s(32, U16),
+    "ta": _s(128, F32), "tb": _s(256, F32), "tc": _s(256, F32), "tm": _s(64, F32),
+    "off0": _s(8, U16), "off1": _s(12, U16), "off2": _s(16, U16), "off3": _s(32, U16),
     "lnt": _s(4, F32), "ys": _s(1024, F32),
     "ps": ("psum", [128, 2048], F32),
 }
-SEMAPHORES = ["ld", "lx", "lw", "v", "s", "t", "gp", "mk", "r0c", "r0s", "r1c", "r1s", "r2c", "r2s", "rn",
-              "cp", "cr", "lo", "yo", "lnd"]
+SEMAPHORES = ["ld", "lx", "lw", "v", "s", "t", "gp", "mk", "r0c", "r0s", "r1c", "r1s", "r2c", "r2s", "rn", "rp",
+              "cr", "c3", "lo", "yo", "lnd"]
 
 
 def wanters(q, b):
@@ -46,12 +45,13 @@ def rank_program(g, core, T, topo):
     q = T.rank_of(core)
     if q is None:
         return
-    A, X, CP = AluOpType, AxisListType.X, ActivationFunctionType.Copy
+    A, X = AluOpType, AxisListType.X
+    CP, ID = ActivationFunctionType.Copy, ActivationFunctionType.Identity
     S = T.sem
     p4, half = q & 3, q >> 2
     own = slice(16 * p4, 16 * p4 + 15)
     queues = {"v": g.vector, "s": g.scalar, "t": g.tensor, "gp": g, "y": g.sync}
-    n, seen = {"v": 0, "s": 0, "t": 0, "gp": 0}, {}
+    n, seen, n_lo = {"v": 0, "s": 0, "t": 0, "gp": 0}, {}, [0]
 
     def need(queue, sem, count):
         if seen.get((queue, sem), 0) < count:
@@ -71,6 +71,7 @@ def rank_program(g, core, T, topo):
 
     ts, tt_, cp = g.vector.tensor_scalar, g.vector.tensor_tensor, g.vector.tensor_copy
     red, tp, scan = g.vector.tensor_reduce, g.vector.transpose, g.vector.tensor_tensor_scan
+    act = g.scalar.activation
 
     def to(d):
         return T.cores[d]
@@ -78,13 +79,21 @@ def rank_program(g, core, T, topo):
     def send(dst, out, in_, sem):
         rid, pid, _ = topo.addr(to(dst))
         g.remote_dma(out, in_, S[sem], S.lo, pid, rid, topo.mask(core, to(dst)))
+        n_lo[0] += len(topo.engines(core, to(dst)))
+
+    def copy(out_q, in_q, out_s, in_s, sem, wq=(), ws=()):
+        for w in wq:
+            need("y", *w)
+        g.sync.dma_start(out_q.bitcast(dt.uint8), in_q.bitcast(dt.uint8)).then_inc(S[sem], 16)
+        for w in ws:
+            need("y", *w)
+        g.sync.dma_start(out_s, in_s).then_inc(S[sem], 16)
 
     for a in range(4):
         for h in range(2):
             e = g.sync if h == 0 else g.scalar
             e.dma_start(T.dmx[32 * a + 16 * h:32 * a + 16 * h + 16, own], T.dm[:, h:h + 15]).then_inc(S.ld, 16)
     g.sync.dma_start(T.xt[:], T.x[:]).then_inc(S.lx, 16)
-    g.scalar.dma_start(T.wt[:], T.w[:]).then_inc(S.lw, 16)
 
     def iota(out, pat, base, cm):
         return done("gp", g.iota(out, pat, base, cm, allow_small_or_imprecise_dtypes=True))
@@ -92,80 +101,76 @@ def rank_program(g, core, T, topo):
     k_pid = done("gp", g.iota(T.pid[:], [[0, 1]], 0, 1))
     k_ir = iota(T.ir[:], [[0, 2], [1, 32]], 0, 0)
     k_dup = iota(T.dupf[:], [[16, 2], [0, 2]], 0, 0)
-    k_c8 = iota(T.c8[:], [[32, 8]], 0, 0)
+    k_c8 = iota(T.c8[:], [[32, 8]], 129, 0)
     k_vraw = iota(T.vraw[:], [[32, 8], [1, 16]], 128, 0)
 
     k_zt = V(g.vector.memset(T.zt[:], 0.0))
-    k_res = V(g.vector.memset(T.res[:], 1.0))
-    V(g.vector.memset(T.tri[:, 32:64], 1.0))
-    k_w0 = V(g.vector.memset(T.win0[:, LB:LB + 128], 128.0))
-    vv(k_res)
-    V(g.vector.memset(T.res[:, 8:40:16], 0.0))
-    V(g.vector.memset(T.res[:, 72:73], 0.0))
+    need("s", "v", k_zt)
+    done("s", act(T.zz[:], T.zt[:, 0:192], CP))
+    done("s", act(T.ones[:], T.zt[:, 0:32], ID, 1.0))
+    k = done("s", act(T.res[:], T.zt[:, 0:104], ID, 1.0))
+    need("s", "s", k)
+    done("s", act(T.res[:, 8:9], T.zt[:, 0:1], CP))
+    done("s", act(T.res[:, 72:73], T.zt[:, 0:1], CP))
+    done("s", act(T.win0[:, LB:LB + 128], T.zt[:, 0:128], ID, 128.0))
+    done("s", act(T.al[:], T.zt[:, 0:128], CP))
+    k_fill0 = done("s", act(T.win1[:, LB:LB + 192], T.zt[:, 0:192], ID, 128.0))
+    done("s", act(T.win2[:, LB:LB + 256], T.zt[:, 0:256], CP))
+    if half == 0:
+        k_fill = done("s", act(T.win3[:, LB:LB + 512], T.zt[:], ID, -1000.0))
+    else:
+        k_fill = done("s", act(T.win3[:, LB + 256:LB + 512], T.zt[:, 0:256], CP))
     need("v", "gp", k_pid)
     for j, m in enumerate((31, 15, 16)):
         k = V(ts(T.pi[:, j:j + 1], T.pid[:], m, None, A.bitwise_and))
     vv(k)
     k = V(cp(T.pf[:, 0:3], T.pi[:, 0:3]))
+    V(g.vector.quantize_mx(T.q2[:, 0:128], T.s2[:, 0:128], T.zt[:]))
     vv(k)
     k = V(ts(T.r32[:, 0:1], T.pf[:, 1:2], 32.0, None, A.mult))
-    need("v", "gp", k_ir)
-    V(ts(T.tri[:, 0:32], T.ir[:, 0:32], T.pf[:, 0:1], None, A.is_gt))
-    vv(k)
-    V(ts(T.fj[:], T.ir[:], T.r32[:, 0:1], None, A.add))
-    V(ts(T.cf[:], T.ir[:], T.r32[:, 0:1], float(1 - LB), A.add, A.add))
     need("v", "gp", k_dup)
     V(ts(T.dup[:], T.dupf[:], T.pf[:, 1:2], None, A.add))
+    V(g.vector.quantize_mx(T.q3[:, 256:384], T.s3[:, 256:384], T.zt[:]))
+    vv(k)
+    V(ts(T.fj[:], T.ir[:], T.r32[:, 0:1], None, A.add))
     need("v", "gp", k_vraw)
     o1, o2 = 128 * (q & 1), 128 * (1 - (q & 1))
     V(ts(T.v1r[:, o1:o1 + 128], T.vraw[:], T.pf[:, 2:3], None, A.add))
     V(ts(T.sel[:, 104 + 8 * p4:112 + 8 * p4], T.c8[:], T.pf[:, 0:1], None, A.add))
-    V(g.vector.memset(T.al[:], 0.0))
-    V(g.vector.memset(T.win1[:, LB:LB + 192], 128.0))
-    V(g.vector.quantize_mx(T.q2[:, 0:128], T.s2[:, 0:128], T.zt[:]))
-    need("s", "v", k_zt)
-    done("s", g.scalar.activation(T.win2[:, LB:LB + 256], T.zt[:, 0:256], CP))
-    k_fill = done("s", g.scalar.activation(T.win3[:, LB:LB + 512], T.zt[:], CP))
 
     peers = [q ^ 1, q ^ 2, q ^ 3]
     g.wait_ge(S.ld, 128)
     m = topo.mask(core, to(peers[0]))
-    for d in peers:
-        m &= topo.mask(core, to(d))
     ids = []
     for d in peers:
+        m &= topo.mask(core, to(d))
         rid, pid, _ = topo.addr(to(d))
         ids.append(DstId(rid=rid, pnc=pid))
     g.remote_dma_fused([RemoteDMATransfer(dst_ids=ids, dma_engine_mask=m, remote_sem=S.mk, srcs=[T.dmx[:, own]],
                                           dsts=[T.dmx[:, own] for d in peers])], local_sem=S.lo)
-    n_lo = 16
-    iota(T.ramp[:, 256:384], [[16, 4], [64, 2], [1, 16]], 384, 0)
-    iota(T.ramp[:, 0:256], [[1, 256]], 128, 0)
-    k_ramp = iota(T.ramp[:, 384:576], [[1, 192]], 512, 0)
+    n_lo[0] += bin(m).count("1")
+    iota(T.ramp[:, 0:1], [[0, 1]], 128, 0)
+    iota(T.ramp[:, 1:129], [[16, 4], [64, 2], [1, 16]], 384, 0)
+    iota(T.ramp[:, 129:385], [[1, 256]], 128, 0)
+    k_ramp = iota(T.ramp[:, 385:577], [[1, 192]], 512, 0)
     if half == 0:
-        k_i128 = iota(T.i128f[:], [[16, 32]], 128, 0)
+        k_gp3 = iota(T.uif[:], [[16, 2], [32, 32]], -256, 0)
 
-    def table(i, count, off, plain=False):
+    def turn(i, count, plain=False):
         win, tr, nb = T["win%d" % i], T["tr%d" % i], count // 32
         vv()
-        k = V(tp(tr[:, 0:count], win[:, LB:LB + count]))
-        vv(k)
-        al = T.al[:, 32 * i:32 * i + 32]
+        vv(V(tp(tr[:, 0:count], win[:, LB:LB + count])))
         dst = T.al[:, 32 * i:32 * i + 32:8] if plain else T.al[:, 32 * i:32 * i + nb]
-        k = V(tt_(dst, tr[:, 0:count:32], tr[:, 16:count:32], A.max))
-        vv(k)
-        k = V(tp(T.ta[:, 32 * i:32 * i + 32], al))
-        vv(k)
-        k = V(cp(T.tb[:, 64 * i:64 * i + 64], T.ta[:, 32 * i:32 * i + 32].indirect(T.dup[:])))
-        vv(k)
-        k = V(tp(T.tc[:, 64 * i:64 * i + 64], T.tb[:, 64 * i:64 * i + 64]))
-        vv(k)
-        if plain:
-            k = V(cp(off[:], T.tc[:, 64 * i:64 * i + 64:8]))
-        else:
-            V(cp(off[:, 0:2 * nb:2], T.tc[:, 64 * i:64 * i + nb]))
-            k = V(cp(off[:, 1:2 * nb:2], T.tc[:, 64 * i + 32:64 * i + 32 + nb]))
-        return k
+        vv(V(tt_(dst, tr[:, 0:count:32], tr[:, 16:count:32], A.max)))
+        vv(V(tp(T.ta[:, 32 * i:32 * i + 32], T.al[:, 32 * i:32 * i + 32])))
+        vv(V(cp(T.tb[:, 64 * i:64 * i + 64], T.ta[:, 32 * i:32 * i + 32].indirect(T.dup[:]))))
+        vv(V(tp(T.tc[:, 64 * i:64 * i + 64], T.tb[:, 64 * i:64 * i + 64])))
+
+    def table(i, count, off):
+        turn(i, count)
+        nb = count // 32
+        V(cp(off[:, 0:2 * nb:2], T.tc[:, 64 * i:64 * i + nb]))
+        return V(cp(off[:, 1:2 * nb:2], T.tc[:, 64 * i + 32:64 * i + 32 + nb]))
 
     def pick(qo, so, qi, si, off, k_off, vwaits=(), swaits=()):
         vv(k_off)
@@ -175,205 +180,198 @@ def rank_program(g, core, T, topo):
         need("s", "v", k_off)
         for w in swaits:
             need("s", *w)
-        return a, done("s", g.scalar.activation(so, si.indirect(off), CP))
+        return a, done("s", act(so, si.indirect(off), CP))
+
+    def lift(out, sel, k):
+        need("s", "v", k)
+        return done("s", act(out, sel, CP, 0.0, float(LB - 1)))
 
     need("v", "ld", 128)
-    k = V(ts(T.and0[:], T.dmx[:, 16 * p4:16 * p4 + 15:2], wanters(q, 0), None, A.bitwise_and))
-    vv(k)
+    vv(V(ts(T.and0[:], T.dmx[:, 16 * p4:16 * p4 + 15:2], wanters(q, 0), None, A.bitwise_and)))
     k = V(ts(T.sel0[:], T.and0[:], 0.0, None, A.is_gt))
+    kb = lift(T.lf0[:], T.sel0[:], k)
     vv(k)
-    k = V(scan(T.inc0[:], T.res[:, 0:8], T.sel0[:], 0.0, A.mult, A.add))
+    need("v", "s", k_fill0)
+    vv(V(scan(T.zz[:, 0:8], T.res[:, 0:8], T.sel0[:], 0.0, A.mult, A.add)))
+    k = V(tp(T.x0t[:], T.zz[:, 0:32]))
+    need("v", "s", kb)
+    ka = V(tt_(T.ya0[:], T.zz[:, 0:8], T.lf0[:], A.add))
     vv(k)
-    k = V(ts(T.x0[:], T.tri[:, 0:32], T.inc0[:, 7:8], None, A.mult))
-    ka = V(tt_(T.ya0[:], T.inc0[:], T.cf[:, 0:8], A.subtract))
-    vv(k)
-    k = V(tp(T.x0t[:], T.x0[:]))
+    k = V(scan(T.zz[:, 65:96], T.ones[:, 0:31], T.x0t[:, 0:31], 0.0, A.mult, A.add))
     vv(ka)
-    ka = V(tt_(T.yb0[:], T.ya0[:], T.sel0[:], A.mult))
+    V(tt_(T.yc0[:], T.ya0[:], T.fj[:, 0:8], A.max))
     vv(k)
-    k = V(red(T.b0[:], T.x0t[:], X, A.add))
-    vv(ka)
-    ka = V(tt_(T.yc0[:], T.yb0[:], T.fj[:, 0:8], A.add))
-    vv(ka)
-    k = V(ts(T.p0[:], T.yc0[:], T.b0[:], None, A.add))
-    vv(k)
+    vv(V(tp(T.bs0[:], T.zz[:, 64:96])))
+    vv(V(ts(T.p0[:], T.yc0[:], T.bs0[:, 7:8], None, A.add)))
     V(cp(T.win0[:].indirect(T.p0[:]), T.v1r[:, o1:o1 + 128]))
     need("v", "lx", 16)
-    k_q = V(g.vector.quantize_mx(T.q0[:, 128:384], T.s0[:, 128:384], T.xt[:]))
-    k_off = table(0, 128, T.off0, plain=True)
+    V(g.vector.quantize_mx(T.q0[:, 128:384], T.s0[:, 128:384], T.xt[:]))
+    turn(0, 128, plain=True)
+    k_off = V(cp(T.off0[:], T.tc[:, 0:64:8]))
     ka, ks = pick(T.slq0[:], T.sls0[:], T.q0[:], T.s0[:], T.off0[:], k_off)
-    need("y", "v", k_q)
-    for dq, ds in ((T.q1, T.s1), (T.q2, T.s2)):
-        g.sync.dma_start(dq[:, 128:384].bitcast(dt.uint8), T.q0[:, 128:384].bitcast(dt.uint8)).then_inc(S.cp, 16)
-        g.sync.dma_start(ds[:, 128:384], T.s0[:, 128:384]).then_inc(S.cp, 16)
+    V(g.vector.quantize_mx(T.q1[:, 128:384], T.s1[:, 128:384], T.xt[:]))
+    V(g.vector.quantize_mx(T.q2[:, 128:384], T.s2[:, 128:384], T.xt[:]))
     need("gp", "v", ka)
     send(q ^ 1, T.q1[:, 384:512].bitcast(dt.uint8), T.slq0[:].bitcast(dt.uint8), "r0c")
     need("gp", "s", ks)
     send(q ^ 1, T.s1[:, 384:512], T.sls0[:], "r0s")
-    n_lo += 32
-    need("y", "r0c", 16)
-    g.sync.dma_start(T.q2[:, 384:512].bitcast(dt.uint8), T.q1[:, 384:512].bitcast(dt.uint8)).then_inc(S.cr, 16)
-    need("y", "r0s", 16)
-    g.sync.dma_start(T.s2[:, 384:512], T.s1[:, 384:512]).then_inc(S.cr, 16)
+    if half == 1:
+        k_gp3 = iota(T.win3[:, LB:LB + 256], [[1, 256]], -256, 0)
+    copy(T.q3[:, 384:640], T.q0[:, 128:384], T.s3[:, 384:640], T.s0[:, 128:384], "c3", (("v", ka),), (("s", ks),))
 
     pa, pb, o = 2 * (p4 >> 1), 2 * (1 - (p4 >> 1)), p4 ^ 1
     need("v", "mk", 48)
     V(ts(T.and1[:, 0:8], T.dmx[:, 16 * o:16 * o + 15:2], wanters(q ^ 1, 0), None, A.bitwise_and))
-    V(ts(T.and1[:, 8:24], T.dmx[:, 16 * pa:16 * pa + 31:2], wanters(q, 1), None, A.bitwise_and))
-    k = V(ts(T.and1[:, 24:40], T.dmx[:, 16 * pb:16 * pb + 31:2], wanters(q ^ 2, 1), None, A.bitwise_and))
+    vv(V(ts(T.and1[:, 8:24], T.dmx[:, 16 * pa:16 * pa + 31:2], wanters(q, 1), None, A.bitwise_and)))
+    k = V(ts(T.sel[:, 0:24], T.and1[:, 0:24], 0.0, None, A.is_gt))
+    kb = lift(T.lf1[:], T.sel[:, 8:24], k)
     vv(k)
-    k = V(ts(T.sel[:, 0:40], T.and1[:, 0:40], 0.0, None, A.is_gt))
+    vv(V(scan(T.zz[:, 32:56], T.res[:, 0:24], T.sel[:, 0:24], 0.0, A.mult, A.add)))
+    k = V(tp(T.x1t[:], T.zz[:, 32:64]))
+    need("v", "s", kb)
+    ka = V(tt_(T.ya1[:], T.zz[:, 40:56], T.lf1[:], A.add))
     vv(k)
-    k = V(scan(T.inc1[:], T.res[:, 0:40], T.sel[:, 0:40], 0.0, A.mult, A.add))
-    vv(k)
-    for j, c in enumerate((7, 23, 39)):
-        k = V(ts(T.x1[:, 32 * j:32 * j + 32], T.tri[:, 0:32], T.inc1[:, c:c + 1], None, A.mult))
-    ka = V(tt_(T.ya1[:], T.inc1[:, 8:24], T.cf[:, 0:16], A.subtract))
-    vv(k)
-    k = V(tp(T.x1t[:], T.x1[:]))
+    k = V(scan(T.zz[:, 97:128], T.ones[:, 0:31], T.x1t[:, 0:31], 0.0, A.mult, A.add))
     vv(ka)
-    ka = V(tt_(T.yb1[:], T.ya1[:], T.sel[:, 8:24], A.mult))
+    ka = V(tt_(T.yc1[:], T.ya1[:], T.fj[:, 0:16], A.max))
     vv(k)
-    k0 = V(red(T.b1[:, 0:1], T.x1t[:, 0:32], X, A.add))
-    V(red(T.b1[:, 1:2], T.x1t[:, 32:64], X, A.add))
-    vv(k0)
-    k0 = V(ts(T.p0k[:], T.inc1[:, 0:8], T.b1[:, 0:1], 255.0, A.add, A.add))
+    vv(V(tp(T.bs1[:], T.zz[:, 96:128])))
+    k0 = V(ts(T.p0k[:], T.zz[:, 32:40], T.bs1[:, 7:8], None, A.add))
     need("s", "v", k0)
     need("s", "gp", k_ramp)
-    ks = done("s", g.scalar.activation(T.v1r[:, o2:o2 + 128], T.ramp[:].indirect(T.p0k[:]), CP))
-    k2 = V(red(T.b1[:, 2:3], T.x1t[:, 64:96], X, A.add))
-    ka = V(tt_(T.yc1[:], T.yb1[:], T.fj[:, 0:16], A.add))
-    V(ts(T.sel[:, 104 + 8 * o:112 + 8 * o], T.inc1[:, 0:8], T.b1[:, 0:1], 255.0, A.add, A.add))
-    vv(ka)
-    k = V(ts(T.p1[:], T.yc1[:], T.b1[:, 1:2], None, A.add))
-    V(ts(T.sel[:, 104 + 8 * pb:120 + 8 * pb], T.inc1[:, 24:40], T.b1[:, 2:3], 383.0, A.add, A.add))
-    vv(k)
+    ks = done("s", act(T.v1r[:, o2:o2 + 128], T.ramp[:].indirect(T.p0k[:]), CP))
+    k_s2 = done("s", act(T.sel[:, 104 + 8 * o:112 + 8 * o], T.zz[:, 32:40], ID, T.bs1[:, 7:8]))
+    k_p1 = V(ts(T.p1[:], T.yc1[:], T.bs1[:, 23:24], None, A.add))
+    V(ts(T.and1[:, 40:72], T.dmx[:, 0:63:2], 1 << (q ^ 4), None, A.bitwise_and))
+    vv(V(ts(T.and1[:, 72:104], T.dmx[:, 0:63:2], 1 << q, None, A.bitwise_and)))
+    V(ts(T.sel[:, 40:104], T.and1[:, 40:104], 0.0, None, A.is_gt))
     need("v", "s", ks)
     V(cp(T.win1[:].indirect(T.p1[:]), T.v1r[:]))
+    need("gp", "v", k_p1)
+    send(q ^ 2, T.p1r[:], T.p1[:], "rp")
+    need("y", "v", k_p1)
+    g.sync.dma_start(T.wt[:], T.w[:]).then_inc(S.lw, 16)
     k_off1 = table(1, 192, T.off1)
-    V(ts(T.and1[:, 40:72], T.dmx[:, 0:63:2], 1 << (q ^ 4), None, A.bitwise_and))
-    k = V(ts(T.and1[:, 72:104], T.dmx[:, 0:63:2], 1 << q, None, A.bitwise_and))
-    vv(k)
-    k = V(ts(T.sel[:, 40:104], T.and1[:, 40:104], 0.0, None, A.is_gt))
-    vv(k)
-    k_tt = V(tp(T.tt[:], T.sel[:, 40:136]))
-    vv(k_tt)
-    k_st = V(cp(T.st[:], T.tt[:, 64:96]))
-    ka, ks = pick(T.slq1[:], T.sls1[:], T.q1[:], T.s1[:], T.off1[:], k_off1,
-                  (("cp", 64), ("r0c", 16)), (("cp", 64), ("r0s", 16)))
+    ka, ks = pick(T.slq1[:], T.sls1[:], T.q1[:], T.s1[:], T.off1[:], k_off1, (("r0c", 16),), (("r0s", 16),))
     need("gp", "v", ka)
     send(q ^ 2, T.q2[:, 512:704].bitcast(dt.uint8), T.slq1[:].bitcast(dt.uint8), "r1c")
     need("gp", "s", ks)
     send(q ^ 2, T.s2[:, 512:704], T.sls1[:], "r1s")
-    n_lo += 32
+    copy(T.q2[:, 384:512], T.q1[:, 384:512], T.s2[:, 384:512], T.s1[:, 384:512], "cr",
+         (("v", ka), ("r0c", 16), ("r0s", 16)), (("s", ks),))
+    copy(T.q3[:, 640:768], T.q1[:, 384:512], T.s3[:, 640:768], T.s1[:, 384:512], "c3")
 
+    need("v", "rp", 16)
+    vv(V(ts(T.sel[:, 104 + 8 * pb:120 + 8 * pb], T.p1r[:], float(385 - LB), 0.0, A.add, A.max)))
+    need("v", "s", k_s2)
+    k_tt = V(tp(T.tt[:], T.sel[:, 40:136]))
+    vv(k_tt)
+    k_st = V(cp(T.st[:], T.tt[:, 64:96]))
     need("s", "v", k_st)
-    k_vr = done("s", g.scalar.activation(T.vr2[:], T.ramp[:].indirect(T.st[:]), CP))
-    k = V(scan(T.inc2[:], T.res[:, 40:104], T.tt[:, 0:64], 0.0, A.mult, A.add))
+    kb = lift(T.lf2[:], T.tt[:, 0:64], k_tt)
+    k_vr = [done("s", act(T.vr2[:, 0:256], T.ramp[:].indirect(T.st[:, 0:16]), CP))]
+    vv(V(scan(T.inc2[:], T.res[:, 40:104], T.tt[:, 0:64], 0.0, A.mult, A.add)))
+    vv(V(tp(T.x2t[:], T.inc2[:])))
+    V(scan(T.zz[:, 129:160], T.ones[:, 0:31], T.x2t[:, 0:31], 0.0, A.mult, A.add))
+    k = V(scan(T.zz[:, 161:192], T.ones[:, 0:31], T.x2t[:, 32:63], 0.0, A.mult, A.add))
+    need("s", "v", k)
+    for c in range(2):
+        b = 32 * c
+        kn = done("s", act(T.tn[:, b:b + 32], T.ones[:], ID, T.x2t[:, b + 31:b + 32], T.zz[:, b + 159:b + 160]))
+    k_vr.append(done("s", act(T.vr2[:, 256:512], T.ramp[:].indirect(T.st[:, 16:32]), CP)))
+    need("v", "s", kb)
+    ka = V(tt_(T.ya2[:], T.inc2[:], T.lf2[:], A.add))
     vv(k)
-    V(ts(T.x2[:, 0:64], T.tri[:], T.inc2[:, 31:32], None, A.mult))
-    k = V(ts(T.x2[:, 64:128], T.tri[:], T.inc2[:, 63:64], None, A.mult))
-    ka = V(tt_(T.ya2[:], T.inc2[:], T.cf[:], A.subtract))
-    vv(k)
-    k = V(tp(T.x2t[:], T.x2[:]))
+    V(tp(T.bs2[:], T.zz[:, 128:192]))
     vv(ka)
-    ka = V(tt_(T.yb2[:], T.ya2[:], T.tt[:, 0:64], A.mult))
-    vv(k)
-    k_n2 = V(red(T.n2o[:], T.x2t[:, 32:64], X, A.add))
-    need("gp", "v", k_n2)
-    send(q ^ 4, T.n2[:], T.n2o[:], "rn")
-    n_lo += 16
-    V(red(T.b2[:], T.x2t[:, 0:32], X, A.add))
-    vv(ka)
-    k = V(tt_(T.yc2[:], T.yb2[:], T.fj[:], A.add))
-    vv(k)
-    k = V(ts(T.p2[:], T.yc2[:, 0:32], T.b2[:], None, A.add))
-    vv(k)
-    need("v", "s", k_vr)
-    V(cp(T.win2[:].indirect(T.p2[:]), T.vr2[:]))
+    vv(V(tt_(T.yc2[:], T.ya2[:], T.fj[:], A.max)))
+    V(ts(T.p2[:], T.yc2[:, 0:32], T.bs2[:, 31:32], None, A.add))
+    for c in range(2):
+        need("v", "s", k_vr[c])
+        vv()
+        V(cp(T.win2[:].indirect(T.p2[:, 16 * c:16 * c + 16]), T.vr2[:, 256 * c:256 * c + 256]))
+        if c == 0:
+            need("v", "s", kn)
+            k_n = V(tp(T.tnt[:], T.tn[:]))
+            need("gp", "v", k_n)
+            send(q ^ 4, T.n2[:], T.tnt[:, 31:32], "rn")
+    nh = T.tnt[:, 63:64]
     k_off2 = table(2, 256, T.off2)
-    ka, ks = pick(T.slq2[:], T.sls2[:], T.q2[:], T.s2[:], T.off2[:], k_off2,
-                  (("cp", 64), ("cr", 32), ("r1c", 16)), (("cp", 64), ("cr", 32), ("r1s", 16)))
+    ka, ks = pick(T.slq2[:], T.sls2[:], T.q2[:], T.s2[:], T.off2[:], k_off2, (("cr", 32), ("r1c", 16)), (("cr", 32), ("r1s", 16)))
     need("gp", "v", ka)
-    send(q ^ 4, T.q3[:, 128:384].bitcast(dt.uint8), T.slq2[:].bitcast(dt.uint8), "r2c")
+    send(q ^ 4, T.q3[:, 0:256].bitcast(dt.uint8), T.slq2[:].bitcast(dt.uint8), "r2c")
     need("gp", "s", ks)
-    send(q ^ 4, T.s3[:, 128:384], T.sls2[:], "r2s")
-    n_lo += 32
-    V(red(T.b3[:], T.x2t[:, 64:96], X, A.add))
-    k = V(red(T.nh[:], T.x2t[:, 96:128], X, A.add))
+    send(q ^ 4, T.s3[:, 0:256], T.sls2[:], "r2s")
+    copy(T.q3[:, 768:960], T.q2[:, 512:704], T.s3[:, 768:960], T.s2[:, 512:704], "c3",
+         (("v", ka), ("r1c", 16), ("r1s", 16)), (("s", ks),))
+
     if half == 0:
-        vv(k)
-        k = V(ts(T.p3[:], T.yc2[:, 32:64], T.b3[:], None, A.add))
+        k = V(ts(T.p3[:], T.yc2[:, 32:64], T.bs2[:, 63:64], None, A.add))
     else:
-        vv(k)
         need("v", "rn", 16)
-        k = V(ts(T.p3[:], T.yc2[:, 32:64], T.b3[:], T.n2[:], A.add, A.add))
+        k = V(ts(T.p3[:], T.yc2[:, 32:64], T.bs2[:, 63:64], T.n2[:], A.add, A.add))
     vv(k)
+    need("v", "s", k_fill)
+    need("v", "gp", k_gp3)
     V(cp(T.win3[:].indirect(T.p3[:]), T.vr2[:]))
+    if half == 0:
+        vv(V(ts(T.ui[:], T.uif[:], T.pf[:, 1:2], None, A.add)))
+        V(ts(T.ub[:], T.ui[:], nh, 0.0, A.subtract, A.min))
+    turn(3, 512)
+    if half == 0:
+        vv(V(tt_(T.tm[:], T.tc[:, 192:256], T.ub[:], A.max)))
+        V(ts(T.off3[:, 0:32:2], T.tm[:, 0:16], 256.0, None, A.add))
+        k_off3 = V(ts(T.off3[:, 1:32:2], T.tm[:, 32:48], 256.0, None, A.add))
+    else:
+        V(cp(T.off3[:, 16:32:2], T.tc[:, 200:208]))
+        V(cp(T.off3[:, 17:32:2], T.tc[:, 232:240]))
+        V(ts(T.off3[:, 0:16:2], T.tc[:, 192:200], 256.0, None, A.add))
+        k_off3 = V(ts(T.off3[:, 1:16:2], T.tc[:, 224:232], 256.0, None, A.add))
     need("v", "lw", 16)
     k_wq = V(g.vector.quantize_mx(T.wq[:], T.ws[:], T.wt[:]))
-    k_off3 = table(3, 512, T.off3)
-    ka, ks = pick(T.qa[:], T.sa[:], T.q2[:], T.s2[:], T.off3[:], k_off3)
 
-    def mm(qx, sx, c, start, stop):
+    def product(c, lo, vwaits, swaits):
+        a, b = 256 * c, 256 * c + 256
+        ka, kb = pick(T.qa[:, a:b], T.sa[:, a:b], T.q3[:, lo:960], T.s3[:, lo:960], T.off3[:, 16 * c:16 * c + 16], k_off3,
+                      vwaits, swaits)
+        need("t", "v", ka)
+        need("t", "s", kb)
         for w in range(2):
-            b = 512 * (2 * w + c)
-            done("t", g.tensor.matmul_mx(T.ps[:, b:b + 256], T.wq[:, 128 * w:128 * w + 128], T.ws[:, 128 * w:128 * w + 128],
-                                         qx, sx, start, stop))
+            done("t", g.tensor.matmul_mx(T.ps[:, 512 * (2 * w + c):512 * (2 * w + c) + 256], T.wq[:, 128 * w:128 * w + 128],
+                                         T.ws[:, 128 * w:128 * w + 128], T.qa[:, a:b], T.sa[:, a:b], True, True))
         return n["t"]
 
     def store(c, k):
-        need("v", "t", k)
+        need("v", "t", k - 1)
         need("s", "t", k)
         a = V(cp(T.ys[:, 256 * c:256 * c + 256], T.ps[:, 512 * c:512 * c + 256]))
-        b = done("s", g.scalar.activation(T.ys[:, 512 + 256 * c:768 + 256 * c], T.ps[:, 1024 + 512 * c:1280 + 512 * c], CP))
+        b = done("s", act(T.ys[:, 512 + 256 * c:768 + 256 * c], T.ps[:, 1024 + 512 * c:1280 + 512 * c], CP))
         need("y", "v", a)
         g.sync.dma_start(T.y[:, 256 * c:256 * c + 256], T.ys[:, 256 * c:256 * c + 256]).then_inc(S.yo, 16)
         need("y", "s", b)
         g.sync.dma_start(T.y[:, 512 + 256 * c:768 + 256 * c], T.ys[:, 512 + 256 * c:768 + 256 * c]).then_inc(S.yo, 16)
 
-    need("t", "v", max(ka, k_wq))
-    need("t", "s", ks)
-    k0 = mm(T.qa[:, 0:256], T.sa[:, 0:256], 0, True, False)
-    k1 = mm(T.qa[:, 256:512], T.sa[:, 256:512], 1, True, half == 1)
+    need("t", "v", k_wq)
+    held, r2 = ("c3", 96), (("r2c", 16), ("r2s", 16))
     if half == 0:
-        need("v", "gp", k_i128)
-        k = V(ts(T.i128[:], T.i128f[:], T.pf[:, 1:2], None, A.add))
-        vv(k)
-        k = V(ts(T.offbf[:], T.i128[:], T.nh[:], 0.0, A.subtract, A.max))
-        vv(k)
-        k_offb = V(ts(T.offb[:], T.offbf[:], 384.0, None, A.min))
-        V(g.vector.quantize_mx(T.q3[:, 0:128], T.s3[:, 0:128], T.zt[:]))
-        k_z = V(g.vector.quantize_mx(T.q3[:, 384:512], T.s3[:, 384:512], T.zt[:]))
-    else:
+        k0 = product(0, 0, (held, r2[0]), (held, r2[1]))
+        k1 = product(1, 0, (), ())
+        store(0, k0)
         store(1, k1)
-    need("v", "rn", 16)
-    k = V(tt_(T.lnt[:, 0:1], T.nh[:], T.n2[:], A.add))
-    k = V(red(T.lnt[:, 1:2], T.x2t[:, 96 + 8 * p4:104 + 8 * p4], X, A.add))
-    need("y", "v", k)
-    g.sync.dma_start(T.ln[:], T.lnt[0:1, 0:2]).then_inc(S.lnd, 16)
-
-    if half == 0:
-        need("s", "v", k_z)
-        vv(k_z)
-        ks = []
-        for c in range(2):
-            a, b = 256 * c, 256 * c + 256
-            ka, kb = pick(T.qb[:, a:b], T.sb8[:, a:b], T.q3[:], T.s3[:], T.offb[:, 16 * c:16 * c + 16], k_offb,
-                          (("r2c", 16),), (("r2s", 16),))
-            need("t", "v", ka)
-            need("t", "s", kb)
-            ks.append(mm(T.qb[:, a:b], T.sb8[:, a:b], c, False, True))
-        store(0, ks[0])
-        store(1, ks[1])
     else:
-        need("t", "r2c", 16)
-        need("t", "r2s", 16)
-        store(0, mm(T.q3[:, 128:384], T.s3[:, 128:384], 0, False, True))
+        k1 = product(1, 256, (held,), (held,))
+        k0 = product(0, 0, (r2[0],), (r2[1],))
+        store(1, k1)
+        store(0, k0)
+    need("v", "rn", 16)
+    V(tt_(T.lnt[:, 0:1], nh, T.n2[:], A.add))
+    k = V(red(T.lnt[:, 1:2], T.x2t[:, 32 + 8 * p4:40 + 8 * p4], X, A.add))
+    need("y", "v", k)
+    g.sync.dma_start(T.ln[:], T.lnt[31:32, 0:2]).then_inc(S.lnd, 16)
 
     for kind in ("v", "s", "t"):
         need("gp", kind, n[kind])
     g.wait_ge(S.gp, n["gp"])
-    g.wait_ge(S.lo, n_lo)
+    g.wait_ge(S.lo, n_lo[0])
     g.wait_ge(S.yo, 64)
     g.wait_ge(S.lnd, 16)

@@ -2,7 +2,8 @@ from concourse.bass import DstId, RemoteDMATransfer
 from concourse.mybir import dt, AluOpType, AxisListType, ActivationFunctionType
 
 F32, I32, BF, U16, U8, Q8 = "float32", "int32", "bfloat16", "uint16", "uint8", "float8_e4m3fn_x4"
-LB = 1024
+LB = 4864
+ZERO = 127
 
 
 def _s(n, d):
@@ -10,31 +11,32 @@ def _s(n, d):
 
 
 SCRATCH = {
-    "dmx": _s(64, I32), "xt": _s(1024, BF), "wt": _s(1024, BF), "zt": _s(512, BF),
+    "dmx": _s(64, I32), "xt": _s(1032, BF), "wt": _s(1024, BF), "zt": _s(512, BF),
     "q0": _s(384, Q8), "s0": _s(384, U8), "q1": _s(512, Q8), "s1": _s(512, U8),
     "q2": _s(704, Q8), "s2": _s(704, U8), "q3": _s(960, Q8), "s3": _s(960, U8),
     "slq0": _s(128, Q8), "sls0": _s(128, U8), "slq1": _s(192, Q8), "sls1": _s(192, U8),
     "slq2": _s(256, Q8), "sls2": _s(256, U8),
     "qa": _s(512, Q8), "sa": _s(512, U8), "wq": _s(256, Q8), "ws": _s(256, U8),
-    "pid": _s(1, I32), "pi": _s(4, I32), "pf": _s(4, F32), "r32": _s(4, F32), "ir": _s(64, F32), "ones": _s(32, F32),
-    "fj": _s(64, F32), "vraw": _s(128, F32), "v1r": _s(256, F32), "dupf": _s(4, F32), "dup": _s(4, U16),
-    "ramp": _s(577, F32), "res": _s(104, F32), "uif": _s(64, F32), "ui": _s(64, F32), "ub": _s(64, F32), "c8": _s(8, F32),
+    "cst": _s(288, F32), "ct": _s(288, F32), "lsh": _s(32, F32), "gl": _s(12, U16), "ones": _s(32, F32), "c8": _s(8, F32),
+    "fj": _s(64, F32), "vraw": _s(128, F32), "v1r": _s(256, F32),
+    "ramp": _s(577, F32), "res": _s(104, F32), "uif": _s(32, F32), "ui": _s(32, F32), "ub": _s(32, F32),
     "zz": _s(192, F32), "and0": _s(8, I32), "sel0": _s(8, F32), "lf0": _s(8, F32), "x0t": _s(32, F32), "bs0": _s(32, F32),
     "ya0": _s(8, F32), "yc0": _s(8, F32), "p0": _s(8, U16),
     "and1": _s(104, I32), "sel": _s(136, F32), "lf1": _s(16, F32), "x1t": _s(32, F32), "bs1": _s(32, F32),
     "ya1": _s(16, F32), "yc1": _s(16, F32), "p0k": _s(8, U16), "p1": _s(16, U16), "p1r": _s(16, U16),
-    "tt": _s(96, F32), "st": _s(32, U16), "vr2": _s(512, F32), "lf2": _s(64, F32), "inc2": _s(64, F32), "x2t": _s(64, F32),
+    "tt": _s(96, F32), "st": _s(16, U16), "vr2": _s(128, F32), "lf2": _s(64, F32), "inc2": _s(64, F32), "x2t": _s(64, F32),
     "bs2": _s(64, F32), "tn": _s(64, F32), "tnt": _s(64, F32), "n2": _s(1, F32),
-    "ya2": _s(64, F32), "yc2": _s(64, F32), "p2": _s(32, U16), "p3": _s(32, U16),
-    "win0": _s(LB + 128, F32), "win1": _s(LB + 192, F32), "win2": _s(LB + 256, F32), "win3": _s(LB + 512, F32),
-    "tr0": _s(128, F32), "tr1": _s(192, F32), "tr2": _s(256, F32), "tr3": _s(512, F32), "al": _s(128, F32),
-    "ta": _s(128, F32), "tb": _s(256, F32), "tc": _s(256, F32), "tm": _s(64, F32),
-    "off0": _s(8, U16), "off1": _s(12, U16), "off2": _s(16, U16), "off3": _s(32, U16),
+    "ya2": _s(64, F32), "yc2": _s(64, F32), "p2": _s(16, U16), "p3": _s(16, U16),
+    "win0": _s(LB + 144, F32), "win1": _s(LB + 208, F32), "win2": _s(LB + 256, F32), "win3": _s(LB + 512, F32),
+    "tr0": _s(288, F32), "tr1": _s(416, F32), "tr2": _s(256, F32), "tr3": _s(512, F32),
+    "m0": _s(16, F32), "m1": _s(16, F32), "z2": _s(64, F32), "h2": _s(32, F32), "m2": _s(16, F32),
+    "z3": _s(128, F32), "h3": _s(64, F32), "m3": _s(32, F32), "tm": _s(32, F32),
+    "off0": _s(16, U16), "off1": _s(16, U16), "off2": _s(16, U16), "off3": _s(32, U16),
     "lnt": _s(4, F32), "ys": _s(1024, F32),
     "ps": ("psum", [128, 2048], F32),
 }
 SEMAPHORES = ["ld", "lx", "lw", "v", "s", "t", "gp", "mk", "r0c", "r0s", "r1c", "r1s", "r2c", "r2s", "rn", "rp",
-              "cr", "c3", "lo", "yo", "lnd"]
+              "c1", "cr", "c3", "d2", "d3", "lo", "yo", "lnd"]
 
 
 def wanters(q, b):
@@ -93,50 +95,34 @@ def rank_program(g, core, T, topo):
         for h in range(2):
             e = g.sync if h == 0 else g.scalar
             e.dma_start(T.dmx[32 * a + 16 * h:32 * a + 16 * h + 16, own], T.dm[:, h:h + 15]).then_inc(S.ld, 16)
-    g.sync.dma_start(T.xt[:], T.x[:]).then_inc(S.lx, 16)
+    g.sync.dma_start(T.xt[:, 8:1032], T.x[:]).then_inc(S.lx, 16)
 
-    def iota(out, pat, base, cm):
+    def iota(out, pat, base, cm=0):
         return done("gp", g.iota(out, pat, base, cm, allow_small_or_imprecise_dtypes=True))
 
-    k_pid = done("gp", g.iota(T.pid[:], [[0, 1]], 0, 1))
-    k_ir = iota(T.ir[:], [[0, 2], [1, 32]], 0, 0)
-    k_dup = iota(T.dupf[:], [[16, 2], [0, 2]], 0, 0)
-    k_c8 = iota(T.c8[:], [[32, 8]], 129, 0)
-    k_vraw = iota(T.vraw[:], [[32, 8], [1, 16]], 128, 0)
+    iota(T.cst[:, 0:16], [[1, 8], [5, 2]], 0)
+    iota(T.cst[:, 16:32], [[1, 8], [-4, 2]], 4)
+    iota(T.cst[:, 32:64], [[16, 2], [0, 16]], 0)
+    k_c1 = iota(T.cst[:, 64:96], [[1, 32]], 0)
+    k_vraw = iota(T.vraw[:], [[32, 8], [1, 16]], 128)
+    k_fj = iota(T.fj[:], [[0, 2], [1, 32]], 0, 32)
 
-    k_zt = V(g.vector.memset(T.zt[:], 0.0))
+    V(g.vector.memset(T.xt[:, 0:8], 0.0))
+    k_zt = V(g.vector.memset(T.zt[:, 0:192], 0.0))
+    V(g.vector.memset(T.zt[:, 192:512], 0.0))
     need("s", "v", k_zt)
     done("s", act(T.zz[:], T.zt[:, 0:192], CP))
     done("s", act(T.ones[:], T.zt[:, 0:32], ID, 1.0))
     k = done("s", act(T.res[:], T.zt[:, 0:104], ID, 1.0))
     need("s", "s", k)
     done("s", act(T.res[:, 8:9], T.zt[:, 0:1], CP))
-    done("s", act(T.res[:, 72:73], T.zt[:, 0:1], CP))
-    done("s", act(T.win0[:, LB:LB + 128], T.zt[:, 0:128], ID, 128.0))
-    done("s", act(T.al[:], T.zt[:, 0:128], CP))
-    k_fill0 = done("s", act(T.win1[:, LB:LB + 192], T.zt[:, 0:192], ID, 128.0))
-    done("s", act(T.win2[:, LB:LB + 256], T.zt[:, 0:256], CP))
-    if half == 0:
-        k_fill = done("s", act(T.win3[:, LB:LB + 512], T.zt[:], ID, -1000.0))
-    else:
-        k_fill = done("s", act(T.win3[:, LB + 256:LB + 512], T.zt[:, 0:256], CP))
-    need("v", "gp", k_pid)
-    for j, m in enumerate((31, 15, 16)):
-        k = V(ts(T.pi[:, j:j + 1], T.pid[:], m, None, A.bitwise_and))
-    vv(k)
-    k = V(cp(T.pf[:, 0:3], T.pi[:, 0:3]))
-    V(g.vector.quantize_mx(T.q2[:, 0:128], T.s2[:, 0:128], T.zt[:]))
-    vv(k)
-    k = V(ts(T.r32[:, 0:1], T.pf[:, 1:2], 32.0, None, A.mult))
-    need("v", "gp", k_dup)
-    V(ts(T.dup[:], T.dupf[:], T.pf[:, 1:2], None, A.add))
-    V(g.vector.quantize_mx(T.q3[:, 256:384], T.s3[:, 256:384], T.zt[:]))
-    vv(k)
-    V(ts(T.fj[:], T.ir[:], T.r32[:, 0:1], None, A.add))
-    need("v", "gp", k_vraw)
+    k_res = done("s", act(T.res[:, 72:73], T.zt[:, 0:1], CP))
+    k_fill0 = done("s", act(T.win0[:, LB - 16:LB + 144], T.zt[:, 0:160], ID, 128.0))
+    need("v", "gp", k_c1)
+    k_ct = V(tp(T.ct[:, 0:96], T.cst[:, 0:96]))
     o1, o2 = 128 * (q & 1), 128 * (1 - (q & 1))
-    V(ts(T.v1r[:, o1:o1 + 128], T.vraw[:], T.pf[:, 2:3], None, A.add))
-    V(ts(T.sel[:, 104 + 8 * p4:112 + 8 * p4], T.c8[:], T.pf[:, 0:1], None, A.add))
+    vv(k_ct)
+    V(cp(T.gl[:, 0:1], T.ct[:, 0:1]))
 
     peers = [q ^ 1, q ^ 2, q ^ 3]
     g.wait_ge(S.ld, 128)
@@ -149,28 +135,40 @@ def rank_program(g, core, T, topo):
     g.remote_dma_fused([RemoteDMATransfer(dst_ids=ids, dma_engine_mask=m, remote_sem=S.mk, srcs=[T.dmx[:, own]],
                                           dsts=[T.dmx[:, own] for d in peers])], local_sem=S.lo)
     n_lo[0] += bin(m).count("1")
-    iota(T.ramp[:, 0:1], [[0, 1]], 128, 0)
-    iota(T.ramp[:, 1:129], [[16, 4], [64, 2], [1, 16]], 384, 0)
-    iota(T.ramp[:, 129:385], [[1, 256]], 128, 0)
-    k_ramp = iota(T.ramp[:, 385:577], [[1, 192]], 512, 0)
-    if half == 0:
-        k_gp3 = iota(T.uif[:], [[16, 2], [32, 32]], -256, 0)
+    k_ramp = iota(T.ramp[:, 129:385], [[1, 256]], 128)
+    k_c8 = iota(T.c8[:], [[32, 8]], 129)
+    k_lsh = iota(T.lsh[:], [[0, 4], [4, 8]], 0, 1)
+    for a, (even, odd) in enumerate(((7, -6), (8, -8), (16, -16), (16, -16))):
+        b = 96 + 32 * a
+        iota(T.cst[:, b:b + 16], [[1, 8], [even, 2]], 8 * (a == 3))
+        k_c2 = iota(T.cst[:, b + 16:b + 32], [[1, 8], [odd, 2]], -odd + 8 * (a == 3))
 
-    def turn(i, count, plain=False):
-        win, tr, nb = T["win%d" % i], T["tr%d" % i], count // 32
+    def turn(i, count):
+        win, tr, mi, nb = T["win%d" % i], T["tr%d" % i], T["m%d" % i], count // 32
         vv()
-        vv(V(tp(tr[:, 0:count], win[:, LB:LB + count])))
-        dst = T.al[:, 32 * i:32 * i + 32:8] if plain else T.al[:, 32 * i:32 * i + nb]
-        vv(V(tt_(dst, tr[:, 0:count:32], tr[:, 16:count:32], A.max)))
-        vv(V(tp(T.ta[:, 32 * i:32 * i + 32], T.al[:, 32 * i:32 * i + 32])))
-        vv(V(cp(T.tb[:, 64 * i:64 * i + 64], T.ta[:, 32 * i:32 * i + 32].indirect(T.dup[:]))))
-        vv(V(tp(T.tc[:, 64 * i:64 * i + 64], T.tb[:, 64 * i:64 * i + 64])))
+        V(tp(tr[:, 0:count], win[:, LB:LB + count]))
+        vv(V(tp(tr[:, count:2 * count + 32], win[:, LB - 16:LB + count + 16])))
+        need("v", "s", k_m0)
+        vv(V(tt_(mi[:, 0:2 * nb + 1], tr[:, 0:2 * count + 32:32], tr[:, 16:2 * count + 32:32], A.max)))
+        return V(cp(T["off%d" % i][:], mi[:].indirect(T.gl[:, 2 * i:2 * i + 1])))
 
-    def table(i, count, off):
-        turn(i, count)
-        nb = count // 32
-        V(cp(off[:, 0:2 * nb:2], T.tc[:, 64 * i:64 * i + nb]))
-        return V(cp(off[:, 1:2 * nb:2], T.tc[:, 64 * i + 32:64 * i + 32 + nb]))
+    def spread(i, count):
+        win, tr, z, nb, sem = T["win%d" % i], T["tr%d" % i], T["z%d" % i], count // 32, "d%d" % i
+        vv()
+        vv(V(tp(tr[:], win[:, LB:LB + count])))
+        k = V(tt_(z[:, 0:nb], tr[:, 0:count:32], tr[:, 16:count:32], A.max))
+        need("y", "v", k)
+        need("s", "v", k)
+        for s in range(1, 8):
+            c, a = slice(nb * s, nb * s + nb), 16 * s
+            g.sync.dma_start(z[0:128 - a, c], z[a:128, 0:nb]).then_inc(S[sem], 16)
+            g.scalar.dma_start(z[128 - a:128, c], z[0:a, 0:nb]).then_inc(S[sem], 16)
+
+    def merge(i, count):
+        z, h, nb = T["z%d" % i], T["h%d" % i], count // 32
+        need("v", "d%d" % i, 224)
+        vv(V(tt_(h[:], z[:, 0:4 * nb], z[:, 4 * nb:8 * nb], A.max)))
+        vv(V(tt_(T["m%d" % i][:], h[:, 0:2 * nb], h[:, 2 * nb:4 * nb], A.max)))
 
     def pick(qo, so, qi, si, off, k_off, vwaits=(), swaits=()):
         vv(k_off)
@@ -190,8 +188,21 @@ def rank_program(g, core, T, topo):
     vv(V(ts(T.and0[:], T.dmx[:, 16 * p4:16 * p4 + 15:2], wanters(q, 0), None, A.bitwise_and)))
     k = V(ts(T.sel0[:], T.and0[:], 0.0, None, A.is_gt))
     kb = lift(T.lf0[:], T.sel0[:], k)
+    need("s", "gp", k_vraw)
+    k_v1 = done("s", act(T.v1r[:, o1:o1 + 128], T.vraw[:], ID, T.ct[:, 32:33]))
+    done("s", act(T.m0[:], T.zt[:, 0:16], CP))
+    k_m0 = done("s", act(T.m1[:], T.zt[:, 0:16], CP))
+    done("s", act(T.win1[:, LB - 16:LB + 208], T.zt[:, 0:224], ID, 128.0))
+    done("s", act(T.win2[:, LB:LB + 256], T.zt[:, 0:256], ID, float(ZERO)))
+    need("s", "gp", k_lsh)
+    done("s", act(T.ramp[:, 0:129], T.ramp[:, 129:258], ID, 255.0))
+    k_rs = done("s", act(T.ramp[:, 385:577], T.ramp[:, 129:321], ID, 384.0))
+    need("s", "s", k_rs)
+    k_rs = done("s", act(T.ramp[:, 0:1], T.zt[:, 0:1], ID, 128.0))
+    done("s", act(T.sel[:, 104 + 8 * p4:112 + 8 * p4], T.c8[:], ID, T.ct[:, 64:65]))
+    k_sh = done("s", act(T.cst[:, 224:256], T.lsh[:], CP, 0.0, 0.25))
     vv(k)
-    need("v", "s", k_fill0)
+    need("v", "s", k_res)
     vv(V(scan(T.zz[:, 0:8], T.res[:, 0:8], T.sel0[:], 0.0, A.mult, A.add)))
     k = V(tp(T.x0t[:], T.zz[:, 0:32]))
     need("v", "s", kb)
@@ -199,25 +210,31 @@ def rank_program(g, core, T, topo):
     vv(k)
     k = V(scan(T.zz[:, 65:96], T.ones[:, 0:31], T.x0t[:, 0:31], 0.0, A.mult, A.add))
     vv(ka)
+    need("v", "gp", k_fj)
     V(tt_(T.yc0[:], T.ya0[:], T.fj[:, 0:8], A.max))
     vv(k)
     vv(V(tp(T.bs0[:], T.zz[:, 64:96])))
-    vv(V(ts(T.p0[:], T.yc0[:], T.bs0[:, 7:8], None, A.add)))
+    k = V(ts(T.p0[:], T.yc0[:], T.bs0[:, 7:8], None, A.add))
+    need("y", "v", k)
+    g.sync.dma_start(T.wt[:], T.w[:]).then_inc(S.lw, 16)
+    vv(k)
+    need("v", "s", k_v1)
     V(cp(T.win0[:].indirect(T.p0[:]), T.v1r[:, o1:o1 + 128]))
     need("v", "lx", 16)
-    V(g.vector.quantize_mx(T.q0[:, 128:384], T.s0[:, 128:384], T.xt[:]))
-    turn(0, 128, plain=True)
-    k_off = V(cp(T.off0[:], T.tc[:, 0:64:8]))
-    ka, ks = pick(T.slq0[:], T.sls0[:], T.q0[:], T.s0[:], T.off0[:], k_off)
-    V(g.vector.quantize_mx(T.q1[:, 128:384], T.s1[:, 128:384], T.xt[:]))
-    V(g.vector.quantize_mx(T.q2[:, 128:384], T.s2[:, 128:384], T.xt[:]))
+    V(g.vector.quantize_mx(T.q0[:, 126:384], T.s0[:, 126:384], T.xt[:]))
+    k_off = turn(0, 128)
+    ka, ks = pick(T.slq0[:], T.sls0[:], T.q0[:], T.s0[:], T.off0[:, 0:8], k_off)
     need("gp", "v", ka)
     send(q ^ 1, T.q1[:, 384:512].bitcast(dt.uint8), T.slq0[:].bitcast(dt.uint8), "r0c")
     need("gp", "s", ks)
     send(q ^ 1, T.s1[:, 384:512], T.sls0[:], "r0s")
-    if half == 1:
-        k_gp3 = iota(T.win3[:, LB:LB + 256], [[1, 256]], -256, 0)
-    copy(T.q3[:, 384:640], T.q0[:, 128:384], T.s3[:, 384:640], T.s0[:, 128:384], "c3", (("v", ka),), (("s", ks),))
+    if half == 0:
+        k_c2 = iota(T.cst[:, 256:288], [[0, 2], [1, 16]], 0)
+        k_gp3 = iota(T.uif[:], [[16, 32]], -256)
+    else:
+        k_gp3 = iota(T.win3[:, LB:LB + 256], [[1, 256]], -256)
+    late = slice(96, 288) if half == 0 else slice(96, 256)
+    copy(T.q1[:, 128:384], T.q0[:, 128:384], T.s1[:, 128:384], T.s0[:, 128:384], "c1", (("v", ka),), (("s", ks),))
 
     pa, pb, o = 2 * (p4 >> 1), 2 * (1 - (p4 >> 1)), p4 ^ 1
     need("v", "mk", 48)
@@ -225,6 +242,10 @@ def rank_program(g, core, T, topo):
     vv(V(ts(T.and1[:, 8:24], T.dmx[:, 16 * pa:16 * pa + 31:2], wanters(q, 1), None, A.bitwise_and)))
     k = V(ts(T.sel[:, 0:24], T.and1[:, 0:24], 0.0, None, A.is_gt))
     kb = lift(T.lf1[:], T.sel[:, 8:24], k)
+    if half == 0:
+        k_fill = done("s", act(T.win3[:, LB:LB + 512], T.zt[:], ID, -1000.0))
+    else:
+        k_fill = done("s", act(T.win3[:, LB + 256:LB + 512], T.zt[:, 0:256], CP))
     vv(k)
     vv(V(scan(T.zz[:, 32:56], T.res[:, 0:24], T.sel[:, 0:24], 0.0, A.mult, A.add)))
     k = V(tp(T.x1t[:], T.zz[:, 32:64]))
@@ -238,21 +259,28 @@ def rank_program(g, core, T, topo):
     vv(V(tp(T.bs1[:], T.zz[:, 96:128])))
     k0 = V(ts(T.p0k[:], T.zz[:, 32:40], T.bs1[:, 7:8], None, A.add))
     need("s", "v", k0)
-    need("s", "gp", k_ramp)
+    need("s", "s", k_rs)
     ks = done("s", act(T.v1r[:, o2:o2 + 128], T.ramp[:].indirect(T.p0k[:]), CP))
     k_s2 = done("s", act(T.sel[:, 104 + 8 * o:112 + 8 * o], T.zz[:, 32:40], ID, T.bs1[:, 7:8]))
     k_p1 = V(ts(T.p1[:], T.yc1[:], T.bs1[:, 23:24], None, A.add))
     V(ts(T.and1[:, 40:72], T.dmx[:, 0:63:2], 1 << (q ^ 4), None, A.bitwise_and))
-    vv(V(ts(T.and1[:, 72:104], T.dmx[:, 0:63:2], 1 << q, None, A.bitwise_and)))
+    k = V(ts(T.and1[:, 72:104], T.dmx[:, 0:63:2], 1 << q, None, A.bitwise_and))
+    need("v", "gp", k_c2)
+    need("v", "s", k_sh)
+    k_ct = V(tp(T.ct[:, late], T.cst[:, late]))
+    vv(k)
     V(ts(T.sel[:, 40:104], T.and1[:, 40:104], 0.0, None, A.is_gt))
+    vv(k_ct)
+    V(cp(T.gl[:, 2:12:2], T.ct[:, 96:256:32]))
     need("v", "s", ks)
     V(cp(T.win1[:].indirect(T.p1[:]), T.v1r[:]))
     need("gp", "v", k_p1)
     send(q ^ 2, T.p1r[:], T.p1[:], "rp")
-    need("y", "v", k_p1)
-    g.sync.dma_start(T.wt[:], T.w[:]).then_inc(S.lw, 16)
-    k_off1 = table(1, 192, T.off1)
-    ka, ks = pick(T.slq1[:], T.sls1[:], T.q1[:], T.s1[:], T.off1[:], k_off1, (("r0c", 16),), (("r0s", 16),))
+    copy(T.q2[:, 126:384], T.q0[:, 126:384], T.s2[:, 126:384], T.s0[:, 126:384], "cr", (("v", k_p1),))
+    copy(T.q3[:, 256:258], T.q0[:, 126:128], T.s3[:, 256:258], T.s0[:, 126:128], "c3")
+    k_off1 = turn(1, 192)
+    ka, ks = pick(T.slq1[:], T.sls1[:], T.q1[:], T.s1[:], T.off1[:, 0:12], k_off1,
+                  (("c1", 32), ("r0c", 16)), (("c1", 32), ("r0s", 16)))
     need("gp", "v", ka)
     send(q ^ 2, T.q2[:, 512:704].bitcast(dt.uint8), T.slq1[:].bitcast(dt.uint8), "r1c")
     need("gp", "s", ks)
@@ -261,16 +289,18 @@ def rank_program(g, core, T, topo):
          (("v", ka), ("r0c", 16), ("r0s", 16)), (("s", ks),))
     copy(T.q3[:, 640:768], T.q1[:, 384:512], T.s3[:, 640:768], T.s1[:, 384:512], "c3")
 
+    share = T.gl[:, 10:11]
     need("v", "rp", 16)
     vv(V(ts(T.sel[:, 104 + 8 * pb:120 + 8 * pb], T.p1r[:], float(385 - LB), 0.0, A.add, A.max)))
     need("v", "s", k_s2)
     k_tt = V(tp(T.tt[:], T.sel[:, 40:136]))
-    vv(k_tt)
-    k_st = V(cp(T.st[:], T.tt[:, 64:96]))
-    need("s", "v", k_st)
     kb = lift(T.lf2[:], T.tt[:, 0:64], k_tt)
-    k_vr = [done("s", act(T.vr2[:, 0:256], T.ramp[:].indirect(T.st[:, 0:16]), CP))]
-    vv(V(scan(T.inc2[:], T.res[:, 40:104], T.tt[:, 0:64], 0.0, A.mult, A.add)))
+    vv(k_tt)
+    ka = V(scan(T.inc2[:], T.res[:, 40:104], T.tt[:, 0:64], 0.0, A.mult, A.add))
+    k_st = V(cp(T.st[:], T.tt[:, 64:96].indirect(share)))
+    need("s", "v", k_st)
+    k_vr = done("s", act(T.vr2[:], T.ramp[:].indirect(T.st[:, 0:8]), CP))
+    vv(ka)
     vv(V(tp(T.x2t[:], T.inc2[:])))
     V(scan(T.zz[:, 129:160], T.ones[:, 0:31], T.x2t[:, 0:31], 0.0, A.mult, A.add))
     k = V(scan(T.zz[:, 161:192], T.ones[:, 0:31], T.x2t[:, 32:63], 0.0, A.mult, A.add))
@@ -278,57 +308,58 @@ def rank_program(g, core, T, topo):
     for c in range(2):
         b = 32 * c
         kn = done("s", act(T.tn[:, b:b + 32], T.ones[:], ID, T.x2t[:, b + 31:b + 32], T.zz[:, b + 159:b + 160]))
-    k_vr.append(done("s", act(T.vr2[:, 256:512], T.ramp[:].indirect(T.st[:, 16:32]), CP)))
     need("v", "s", kb)
     ka = V(tt_(T.ya2[:], T.inc2[:], T.lf2[:], A.add))
     vv(k)
     V(tp(T.bs2[:], T.zz[:, 128:192]))
+    need("v", "s", kn)
+    k_n = V(tp(T.tnt[:], T.tn[:]))
+    nh = T.tnt[:, 63:64]
+    need("gp", "v", k_n)
+    send(q ^ 4, T.n2[:], T.tnt[:, 31:32], "rn")
     vv(ka)
     vv(V(tt_(T.yc2[:], T.ya2[:], T.fj[:], A.max)))
-    V(ts(T.p2[:], T.yc2[:, 0:32], T.bs2[:, 31:32], None, A.add))
-    for c in range(2):
-        need("v", "s", k_vr[c])
-        vv()
-        V(cp(T.win2[:].indirect(T.p2[:, 16 * c:16 * c + 16]), T.vr2[:, 256 * c:256 * c + 256]))
-        if c == 0:
-            need("v", "s", kn)
-            k_n = V(tp(T.tnt[:], T.tn[:]))
-            need("gp", "v", k_n)
-            send(q ^ 4, T.n2[:], T.tnt[:, 31:32], "rn")
-    nh = T.tnt[:, 63:64]
-    k_off2 = table(2, 256, T.off2)
-    ka, ks = pick(T.slq2[:], T.sls2[:], T.q2[:], T.s2[:], T.off2[:], k_off2, (("cr", 32), ("r1c", 16)), (("cr", 32), ("r1s", 16)))
+    vv(V(ts(T.p2[:], T.yc2[:, 0:32].indirect(share), T.bs2[:, 31:32], None, A.add)))
+    need("v", "s", k_vr)
+    V(cp(T.win2[:].indirect(T.p2[:, 0:8]), T.vr2[:]))
+    spread(2, 256)
+    if half == 0:
+        k = V(ts(T.p3[:], T.yc2[:, 32:64].indirect(share), T.bs2[:, 63:64], None, A.add))
+    else:
+        need("v", "rn", 16)
+        k = V(ts(T.p3[:], T.yc2[:, 32:64].indirect(share), T.bs2[:, 63:64], T.n2[:], A.add, A.add))
+    vv(k)
+    need("v", "s", k_fill)
+    need("v", "gp", k_gp3)
+    V(cp(T.win3[:].indirect(T.p3[:, 0:8]), T.vr2[:]))
+    spread(3, 512)
+    copy(T.q3[:, 768:960], T.q2[:, 512:704], T.s3[:, 768:960], T.s2[:, 512:704], "c3", (("r1c", 16), ("r1s", 16)))
+    merge(2, 256)
+    k_off2 = V(cp(T.off2[:], T.m2[:].indirect(T.gl[:, 4:5])))
+    ka, ks = pick(T.slq2[:], T.sls2[:], T.q2[:], T.s2[:], T.off2[:], k_off2, (("cr", 64), ("r1c", 16)), (("cr", 64), ("r1s", 16)))
     need("gp", "v", ka)
     send(q ^ 4, T.q3[:, 0:256].bitcast(dt.uint8), T.slq2[:].bitcast(dt.uint8), "r2c")
     need("gp", "s", ks)
     send(q ^ 4, T.s3[:, 0:256], T.sls2[:], "r2s")
-    copy(T.q3[:, 768:960], T.q2[:, 512:704], T.s3[:, 768:960], T.s2[:, 512:704], "c3",
-         (("v", ka), ("r1c", 16), ("r1s", 16)), (("s", ks),))
 
-    if half == 0:
-        k = V(ts(T.p3[:], T.yc2[:, 32:64], T.bs2[:, 63:64], None, A.add))
-    else:
-        need("v", "rn", 16)
-        k = V(ts(T.p3[:], T.yc2[:, 32:64], T.bs2[:, 63:64], T.n2[:], A.add, A.add))
-    vv(k)
-    need("v", "s", k_fill)
-    need("v", "gp", k_gp3)
-    V(cp(T.win3[:].indirect(T.p3[:]), T.vr2[:]))
-    if half == 0:
-        vv(V(ts(T.ui[:], T.uif[:], T.pf[:, 1:2], None, A.add)))
-        V(ts(T.ub[:], T.ui[:], nh, 0.0, A.subtract, A.min))
-    turn(3, 512)
-    if half == 0:
-        vv(V(tt_(T.tm[:], T.tc[:, 192:256], T.ub[:], A.max)))
-        V(ts(T.off3[:, 0:32:2], T.tm[:, 0:16], 256.0, None, A.add))
-        k_off3 = V(ts(T.off3[:, 1:32:2], T.tm[:, 32:48], 256.0, None, A.add))
-    else:
-        V(cp(T.off3[:, 16:32:2], T.tc[:, 200:208]))
-        V(cp(T.off3[:, 17:32:2], T.tc[:, 232:240]))
-        V(ts(T.off3[:, 0:16:2], T.tc[:, 192:200], 256.0, None, A.add))
-        k_off3 = V(ts(T.off3[:, 1:16:2], T.tc[:, 224:232], 256.0, None, A.add))
+    V(g.vector.quantize_mx(T.q3[:, 384:640], T.s3[:, 384:640], T.xt[:, 8:1032]))
     need("v", "lw", 16)
     k_wq = V(g.vector.quantize_mx(T.wq[:], T.ws[:], T.wt[:]))
+    if half == 0:
+        need("s", "gp", k_gp3)
+        need("s", "v", k_ct)
+        ku = done("s", act(T.ui[:], T.uif[:], ID, T.ct[:, 256:257]))
+        need("v", "s", ku)
+        V(ts(T.ub[:], T.ui[:], nh, 0.0, A.subtract, A.min))
+    merge(3, 512)
+    if half == 0:
+        for c in range(2):
+            k = V(tt_(T.tm[:, 16 * c:16 * c + 16], T.m3[:].indirect(T.gl[:, 6 + 2 * c:7 + 2 * c]), T.ub[:, 16 * c:16 * c + 16], A.max))
+        vv(k)
+        k_off3 = V(ts(T.off3[:], T.tm[:], 256.0, None, A.add))
+    else:
+        V(cp(T.off3[:, 16:32], T.m3[:].indirect(T.gl[:, 8:9])))
+        k_off3 = V(ts(T.off3[:, 0:16], T.m3[:].indirect(T.gl[:, 6:7]), 256.0, None, A.add))
 
     def product(c, lo, vwaits, swaits):
         a, b = 256 * c, 256 * c + 256
@@ -351,22 +382,26 @@ def rank_program(g, core, T, topo):
         need("y", "s", b)
         g.sync.dma_start(T.y[:, 512 + 256 * c:768 + 256 * c], T.ys[:, 512 + 256 * c:768 + 256 * c]).then_inc(S.yo, 16)
 
+    def lengths():
+        need("v", "rn", 16)
+        V(ts(T.lnt[:, 0:1], nh, T.n2[:], None, A.add))
+        return V(red(T.lnt[:, 1:2], T.x2t[:, 32 + 8 * p4:40 + 8 * p4], X, A.add))
+
     need("t", "v", k_wq)
     held, r2 = ("c3", 96), (("r2c", 16), ("r2s", 16))
     if half == 0:
         k0 = product(0, 0, (held, r2[0]), (held, r2[1]))
         k1 = product(1, 0, (), ())
         store(0, k0)
+        k_ln = lengths()
         store(1, k1)
     else:
         k1 = product(1, 256, (held,), (held,))
         k0 = product(0, 0, (r2[0],), (r2[1],))
         store(1, k1)
+        k_ln = lengths()
         store(0, k0)
-    need("v", "rn", 16)
-    V(tt_(T.lnt[:, 0:1], nh, T.n2[:], A.add))
-    k = V(red(T.lnt[:, 1:2], T.x2t[:, 32 + 8 * p4:40 + 8 * p4], X, A.add))
-    need("y", "v", k)
+    need("y", "v", k_ln)
     g.sync.dma_start(T.ln[:], T.lnt[31:32, 0:2]).then_inc(S.lnd, 16)
 
     for kind in ("v", "s", "t"):

@@ -17,26 +17,27 @@ SCRATCH = {
     "slq0": _s(128, Q8), "sls0": _s(128, U8), "slq1": _s(192, Q8), "sls1": _s(192, U8),
     "slq2": _s(256, Q8), "sls2": _s(256, U8),
     "qa": _s(512, Q8), "sa": _s(512, U8), "wq": _s(256, Q8), "ws": _s(256, U8),
-    "cst": _s(288, F32), "ct": _s(288, F32), "lsh": _s(32, F32), "gl": _s(12, U16), "ones": _s(32, F32), "c8": _s(8, F32),
-    "fj": _s(64, F32), "vraw": _s(128, F32), "v1r": _s(256, F32),
+    "pa": _s(1, I32), "pb": _s(1, I32), "bi": _s(8, I32), "bf": _s(8, F32), "c5": _s(1, F32),
+    "gl": _s(12, U16), "ones": _s(32, F32), "c8": _s(8, F32),
+    "fj": _s(64, F32), "vraw": _s(128, F32), "v1r": _s(128, F32),
     "ramp": _s(577, F32), "res": _s(104, F32), "uif": _s(32, F32), "ui": _s(32, F32), "ub": _s(32, F32),
-    "zz": _s(192, F32), "and0": _s(8, I32), "sel0": _s(8, F32), "lf0": _s(8, F32), "x0t": _s(32, F32), "bs0": _s(32, F32),
+    "zz": _s(200, F32), "and0": _s(8, I32), "sel0": _s(8, F32), "lf0": _s(8, F32), "x0t": _s(32, F32), "bs0": _s(32, F32),
     "ya0": _s(8, F32), "yc0": _s(8, F32), "p0": _s(8, U16),
     "and1": _s(104, I32), "sel": _s(136, F32), "lf1": _s(16, F32), "x1t": _s(32, F32), "bs1": _s(32, F32),
-    "ya1": _s(16, F32), "yc1": _s(16, F32), "p0k": _s(8, U16), "p1": _s(16, U16), "p1r": _s(16, U16),
+    "ya1": _s(16, F32), "yc1": _s(16, F32), "p1": _s(16, U16), "st1": _s(16, U16), "vr1": _s(64, F32),
     "tt": _s(96, F32), "st": _s(16, U16), "vr2": _s(128, F32), "lf2": _s(64, F32), "inc2": _s(64, F32), "x2t": _s(64, F32),
     "bs2": _s(64, F32), "tn": _s(64, F32), "tnt": _s(64, F32), "n2": _s(1, F32),
     "ya2": _s(64, F32), "yc2": _s(64, F32), "p2": _s(16, U16), "p3": _s(16, U16),
-    "win0": _s(LB + 144, F32), "win1": _s(LB + 208, F32), "win2": _s(LB + 256, F32), "win3": _s(LB + 512, F32),
-    "tr0": _s(288, F32), "tr1": _s(416, F32), "tr2": _s(256, F32), "tr3": _s(512, F32),
-    "m0": _s(16, F32), "m1": _s(16, F32), "z2": _s(64, F32), "h2": _s(32, F32), "m2": _s(16, F32),
+    "win0": _s(LB + 144, F32), "win1": _s(LB + 192, F32), "win2": _s(LB + 256, F32), "win3": _s(LB + 512, F32),
+    "tr0": _s(288, F32), "tr1": _s(192, F32), "tr2": _s(256, F32), "tr3": _s(512, F32),
+    "m01": _s(32, F32), "z1": _s(48, F32), "h1": _s(24, F32), "z2": _s(64, F32), "h2": _s(32, F32), "m2": _s(16, F32),
     "z3": _s(128, F32), "h3": _s(64, F32), "m3": _s(32, F32), "tm": _s(32, F32),
     "off0": _s(16, U16), "off1": _s(16, U16), "off2": _s(16, U16), "off3": _s(32, U16),
     "lnt": _s(4, F32), "ys": _s(1024, F32),
-    "ps": ("psum", [128, 2048], F32),
+    "ps": ("psum", [128, 4096], F32),
 }
-SEMAPHORES = ["ld", "lx", "lw", "v", "s", "t", "gp", "mk", "r0c", "r0s", "r1c", "r1s", "r2c", "r2s", "rn", "rp",
-              "c1", "cr", "c3", "d2", "d3", "lo", "yo", "lnd"]
+SEMAPHORES = ["ld", "lx", "lw", "v", "s", "t", "gp", "mk", "r0c", "r0s", "r1c", "r1s", "r2c", "r2s", "rn",
+              "c1", "cr", "c3", "d1", "d2", "d3", "lo", "yo", "lnd"]
 
 
 def wanters(q, b):
@@ -53,7 +54,7 @@ def rank_program(g, core, T, topo):
     p4, half = q & 3, q >> 2
     own = slice(16 * p4, 16 * p4 + 15)
     queues = {"v": g.vector, "s": g.scalar, "t": g.tensor, "gp": g, "y": g.sync}
-    n, seen, n_lo = {"v": 0, "s": 0, "t": 0, "gp": 0}, {}, [0]
+    n, seen, n_lo, n_yo = {"v": 0, "s": 0, "t": 0, "gp": 0}, {}, [0], [0]
 
     def need(queue, sem, count):
         if seen.get((queue, sem), 0) < count:
@@ -100,29 +101,33 @@ def rank_program(g, core, T, topo):
     def iota(out, pat, base, cm=0):
         return done("gp", g.iota(out, pat, base, cm, allow_small_or_imprecise_dtypes=True))
 
-    iota(T.cst[:, 0:16], [[1, 8], [5, 2]], 0)
-    iota(T.cst[:, 16:32], [[1, 8], [-4, 2]], 4)
-    iota(T.cst[:, 32:64], [[16, 2], [0, 16]], 0)
-    k_c1 = iota(T.cst[:, 64:96], [[1, 32]], 0)
+    k_pa = done("gp", g.iota(T.pa[:], [[0, 1]], 0, 129))
+    k_pb = done("gp", g.iota(T.pb[:], [[0, 1]], 0, 17))
     k_vraw = iota(T.vraw[:], [[32, 8], [1, 16]], 128)
     k_fj = iota(T.fj[:], [[0, 2], [1, 32]], 0, 32)
 
-    V(g.vector.memset(T.xt[:, 0:8], 0.0))
-    k_zt = V(g.vector.memset(T.zt[:, 0:192], 0.0))
-    V(g.vector.memset(T.zt[:, 192:512], 0.0))
+    k_zt = V(g.vector.memset(T.zt[:, 0:208], 0.0))
     need("s", "v", k_zt)
-    done("s", act(T.zz[:], T.zt[:, 0:192], CP))
     done("s", act(T.ones[:], T.zt[:, 0:32], ID, 1.0))
-    k = done("s", act(T.res[:], T.zt[:, 0:104], ID, 1.0))
-    need("s", "s", k)
-    done("s", act(T.res[:, 8:9], T.zt[:, 0:1], CP))
-    k_res = done("s", act(T.res[:, 72:73], T.zt[:, 0:1], CP))
-    k_fill0 = done("s", act(T.win0[:, LB - 16:LB + 144], T.zt[:, 0:160], ID, 128.0))
-    need("v", "gp", k_c1)
-    k_ct = V(tp(T.ct[:, 0:96], T.cst[:, 0:96]))
-    o1, o2 = 128 * (q & 1), 128 * (1 - (q & 1))
-    vv(k_ct)
-    V(cp(T.gl[:, 0:1], T.ct[:, 0:1]))
+    k_zz = done("s", act(T.zz[:], T.zt[:, 0:200], CP))
+    done("s", act(T.win0[:, LB - 16:LB + 144], T.zt[:, 0:160], ID, 128.0))
+    k_m0 = done("s", act(T.m01[:], T.zt[:, 0:32], CP))
+
+    def bits(c, src, shift, mask):
+        need("v", "gp", k_pb if c == 1 else k_pa)
+        if shift:
+            return V(ts(T.bi[:, c:c + 1], src[:], shift, mask, A.logical_shift_right, A.bitwise_and))
+        return V(ts(T.bi[:, c:c + 1], src[:], mask, None, A.bitwise_and))
+
+    bits(0, T.pa, 0, 16)
+    bits(2, T.pa, 1, 7)
+    bits(3, T.pa, 0, 31)
+    bits(4, T.pa, 0, 15)
+    k_bi = bits(1, T.pb, 4, 1)
+    V(g.vector.memset(T.xt[:, 0:8], 0.0))
+    vv(k_bi)
+    k_bf = V(cp(T.bf[:, 0:5], T.bi[:, 0:5]))
+    ei = T.bf[:, 2:3]
 
     peers = [q ^ 1, q ^ 2, q ^ 3]
     g.wait_ge(S.ld, 128)
@@ -135,27 +140,19 @@ def rank_program(g, core, T, topo):
     g.remote_dma_fused([RemoteDMATransfer(dst_ids=ids, dma_engine_mask=m, remote_sem=S.mk, srcs=[T.dmx[:, own]],
                                           dsts=[T.dmx[:, own] for d in peers])], local_sem=S.lo)
     n_lo[0] += bin(m).count("1")
-    k_ramp = iota(T.ramp[:, 129:385], [[1, 256]], 128)
     k_c8 = iota(T.c8[:], [[32, 8]], 129)
-    k_lsh = iota(T.lsh[:], [[0, 4], [4, 8]], 0, 1)
-    for a, (even, odd) in enumerate(((7, -6), (8, -8), (16, -16), (16, -16))):
-        b = 96 + 32 * a
-        iota(T.cst[:, b:b + 16], [[1, 8], [even, 2]], 8 * (a == 3))
-        k_c2 = iota(T.cst[:, b + 16:b + 32], [[1, 8], [odd, 2]], -odd + 8 * (a == 3))
+    k_ramp = iota(T.ramp[:, 129:385], [[1, 256]], 128)
+    if half == 0:
+        k_gp3 = iota(T.uif[:], [[16, 32]], -256)
+    else:
+        k_gp3 = iota(T.win3[:, LB:LB + 256], [[1, 256]], -256)
 
     def turn(i, count):
-        win, tr, mi, nb = T["win%d" % i], T["tr%d" % i], T["m%d" % i], count // 32
-        vv()
-        V(tp(tr[:, 0:count], win[:, LB:LB + count]))
-        vv(V(tp(tr[:, count:2 * count + 32], win[:, LB - 16:LB + count + 16])))
-        need("v", "s", k_m0)
-        vv(V(tt_(mi[:, 0:2 * nb + 1], tr[:, 0:2 * count + 32:32], tr[:, 16:2 * count + 32:32], A.max)))
-        return V(cp(T["off%d" % i][:], mi[:].indirect(T.gl[:, 2 * i:2 * i + 1])))
+        return V(tp(T["tr%d" % i][:], T["win%d" % i][:, LB:LB + count]))
 
-    def spread(i, count):
-        win, tr, z, nb, sem = T["win%d" % i], T["tr%d" % i], T["z%d" % i], count // 32, "d%d" % i
-        vv()
-        vv(V(tp(tr[:], win[:, LB:LB + count])))
+    def spread(i, count, k):
+        tr, z, nb, sem = T["tr%d" % i], T["z%d" % i], count // 32, "d%d" % i
+        vv(k)
         k = V(tt_(z[:, 0:nb], tr[:, 0:count:32], tr[:, 16:count:32], A.max))
         need("y", "v", k)
         need("s", "v", k)
@@ -164,11 +161,17 @@ def rank_program(g, core, T, topo):
             g.sync.dma_start(z[0:128 - a, c], z[a:128, 0:nb]).then_inc(S[sem], 16)
             g.scalar.dma_start(z[128 - a:128, c], z[0:a, 0:nb]).then_inc(S[sem], 16)
 
-    def merge(i, count):
+    def merge(i, count, out, fill=()):
         z, h, nb = T["z%d" % i], T["h%d" % i], count // 32
         need("v", "d%d" % i, 224)
-        vv(V(tt_(h[:], z[:, 0:4 * nb], z[:, 4 * nb:8 * nb], A.max)))
-        vv(V(tt_(T["m%d" % i][:], h[:, 0:2 * nb], h[:, 2 * nb:4 * nb], A.max)))
+        k = V(tt_(h[:], z[:, 0:4 * nb], z[:, 4 * nb:8 * nb], A.max))
+        if fill:
+            fill[0]()
+        vv(k)
+        k = V(tt_(out, h[:, 0:2 * nb], h[:, 2 * nb:4 * nb], A.max))
+        if fill:
+            fill[1]()
+        vv(k)
 
     def pick(qo, so, qi, si, off, k_off, vwaits=(), swaits=()):
         vv(k_off)
@@ -184,157 +187,196 @@ def rank_program(g, core, T, topo):
         need("s", "v", k)
         return done("s", act(out, sel, CP, 0.0, float(LB - 1)))
 
+    def last_gather(c, nb):
+        return V(ts(T.gl[:, c:c + 1], T.bf[:, 1:2], nb, ei, A.mult, A.add))
+
     need("v", "ld", 128)
-    vv(V(ts(T.and0[:], T.dmx[:, 16 * p4:16 * p4 + 15:2], wanters(q, 0), None, A.bitwise_and)))
+    k = V(ts(T.and0[:], T.dmx[:, 16 * p4:16 * p4 + 15:2], wanters(q, 0), None, A.bitwise_and))
+    bits(5, T.pa, 5, 15)
+    vv(k)
     k = V(ts(T.sel0[:], T.and0[:], 0.0, None, A.is_gt))
     kb = lift(T.lf0[:], T.sel0[:], k)
+    k_bi = bits(6, T.pa, 5, 31)
+    need("s", "v", k_bf)
     need("s", "gp", k_vraw)
-    k_v1 = done("s", act(T.v1r[:, o1:o1 + 128], T.vraw[:], ID, T.ct[:, 32:33]))
-    done("s", act(T.m0[:], T.zt[:, 0:16], CP))
-    k_m0 = done("s", act(T.m1[:], T.zt[:, 0:16], CP))
-    done("s", act(T.win1[:, LB - 16:LB + 208], T.zt[:, 0:224], ID, 128.0))
-    done("s", act(T.win2[:, LB:LB + 256], T.zt[:, 0:256], ID, float(ZERO)))
-    need("s", "gp", k_lsh)
-    done("s", act(T.ramp[:, 0:129], T.ramp[:, 129:258], ID, 255.0))
-    k_rs = done("s", act(T.ramp[:, 385:577], T.ramp[:, 129:321], ID, 384.0))
-    need("s", "s", k_rs)
-    k_rs = done("s", act(T.ramp[:, 0:1], T.zt[:, 0:1], ID, 128.0))
-    done("s", act(T.sel[:, 104 + 8 * p4:112 + 8 * p4], T.c8[:], ID, T.ct[:, 64:65]))
-    k_sh = done("s", act(T.cst[:, 224:256], T.lsh[:], CP, 0.0, 0.25))
+    k_v1 = done("s", act(T.v1r[:], T.vraw[:], ID, T.bf[:, 0:1]))
+    k1 = done("s", act(T.res[:], T.zt[:, 0:104], ID, 1.0))
     vv(k)
-    need("v", "s", k_res)
-    vv(V(scan(T.zz[:, 0:8], T.res[:, 0:8], T.sel0[:], 0.0, A.mult, A.add)))
+    need("v", "s", k_zz)
+    k = V(scan(T.zz[:, 0:8], T.ones[:, 0:8], T.sel0[:], 0.0, A.mult, A.add))
+    vv(k_bf)
+    k_c5 = V(ts(T.c5[:], T.bf[:, 0:1], -0.0625, 5.0, A.mult, A.add))
+    vv(k)
     k = V(tp(T.x0t[:], T.zz[:, 0:32]))
     need("v", "s", kb)
     ka = V(tt_(T.ya0[:], T.zz[:, 0:8], T.lf0[:], A.add))
     vv(k)
-    k = V(scan(T.zz[:, 65:96], T.ones[:, 0:31], T.x0t[:, 0:31], 0.0, A.mult, A.add))
+    k = V(scan(T.zz[:, 73:104], T.ones[:, 0:31], T.x0t[:, 0:31], 0.0, A.mult, A.add))
     vv(ka)
     need("v", "gp", k_fj)
     V(tt_(T.yc0[:], T.ya0[:], T.fj[:, 0:8], A.max))
     vv(k)
-    vv(V(tp(T.bs0[:], T.zz[:, 64:96])))
+    k = V(tp(T.bs0[:], T.zz[:, 72:104]))
+    V(cp(T.gl[:, 8:12:2], T.bi[:, 5:7]))
+    vv(k)
     k = V(ts(T.p0[:], T.yc0[:], T.bs0[:, 7:8], None, A.add))
+    V(ts(T.gl[:, 0:1], T.bf[:, 1:2], T.c5[:], ei, A.mult, A.add))
     need("y", "v", k)
     g.sync.dma_start(T.wt[:], T.w[:]).then_inc(S.lw, 16)
     vv(k)
     need("v", "s", k_v1)
-    V(cp(T.win0[:].indirect(T.p0[:]), T.v1r[:, o1:o1 + 128]))
+    k_w0 = V(cp(T.win0[:].indirect(T.p0[:]), T.v1r[:]))
     need("v", "lx", 16)
     V(g.vector.quantize_mx(T.q0[:, 126:384], T.s0[:, 126:384], T.xt[:]))
-    k_off = turn(0, 128)
-    ka, ks = pick(T.slq0[:], T.sls0[:], T.q0[:], T.s0[:], T.off0[:, 0:8], k_off)
-    need("gp", "v", ka)
+    need("s", "s", k1)
+    done("s", act(T.res[:, 16:33:16], T.zt[:, 0:2], CP))
+    done("s", act(T.res[:, 72:73], T.zt[:, 0:1], CP))
+    need("s", "gp", k_c8)
+    k_res = done("s", act(T.sel[:, 104 + 8 * p4:112 + 8 * p4], T.c8[:], ID, T.bf[:, 3:4]))
+    need("s", "gp", k_ramp)
+    done("s", act(T.ramp[:, 0:129], T.ramp[:, 129:258], ID, 255.0))
+    k_rs = done("s", act(T.ramp[:, 385:577], T.ramp[:, 129:321], ID, 384.0))
+    k_ui = done("s", act(T.win1[:, LB:LB + 192], T.zt[:, 0:192], ID, 128.0))
+    if half == 0:
+        need("s", "gp", k_gp3)
+        k_ui = done("s", act(T.ui[:], T.uif[:], ID, T.bf[:, 4:5]))
+    vv(k_w0)
+    V(tp(T.tr0[:, 0:128], T.win0[:, LB:LB + 128]))
+    k0 = V(tp(T.tr0[:, 128:288], T.win0[:, LB - 16:LB + 144]))
+    last_gather(2, 6.0)
+    last_gather(4, 8.0)
+    vv(k0)
+    need("v", "s", k_m0)
+    k0 = V(tt_(T.m01[:, 0:9], T.tr0[:, 0:288:32], T.tr0[:, 16:288:32], A.max))
+    last_gather(6, 16.0)
+    vv(k0)
+    k0 = V(cp(T.off0[:], T.m01[:, 0:16].indirect(T.gl[:, 0:1])))
+    V(g.vector.memset(T.zt[:, 208:512], 0.0))
+    k0, ks = pick(T.slq0[:], T.sls0[:], T.q0[:], T.s0[:], T.off0[:, 0:8], k0)
+    need("gp", "v", k0)
     send(q ^ 1, T.q1[:, 384:512].bitcast(dt.uint8), T.slq0[:].bitcast(dt.uint8), "r0c")
     need("gp", "s", ks)
     send(q ^ 1, T.s1[:, 384:512], T.sls0[:], "r0s")
-    if half == 0:
-        k_c2 = iota(T.cst[:, 256:288], [[0, 2], [1, 16]], 0)
-        k_gp3 = iota(T.uif[:], [[16, 32]], -256)
-    else:
-        k_gp3 = iota(T.win3[:, LB:LB + 256], [[1, 256]], -256)
-    late = slice(96, 288) if half == 0 else slice(96, 256)
-    copy(T.q1[:, 128:384], T.q0[:, 128:384], T.s1[:, 128:384], T.s0[:, 128:384], "c1", (("v", ka),), (("s", ks),))
+    copy(T.q1[:, 128:384], T.q0[:, 128:384], T.s1[:, 128:384], T.s0[:, 128:384], "c1", (("v", k0),), (("s", ks),))
 
     pa, pb, o = 2 * (p4 >> 1), 2 * (1 - (p4 >> 1)), p4 ^ 1
+    share1, share = T.gl[:, 8:9], T.gl[:, 10:11]
     need("v", "mk", 48)
-    V(ts(T.and1[:, 0:8], T.dmx[:, 16 * o:16 * o + 15:2], wanters(q ^ 1, 0), None, A.bitwise_and))
-    vv(V(ts(T.and1[:, 8:24], T.dmx[:, 16 * pa:16 * pa + 31:2], wanters(q, 1), None, A.bitwise_and)))
-    k = V(ts(T.sel[:, 0:24], T.and1[:, 0:24], 0.0, None, A.is_gt))
-    kb = lift(T.lf1[:], T.sel[:, 8:24], k)
+    V(ts(T.and1[:, 0:16], T.dmx[:, 16 * pa:16 * pa + 31:2], wanters(q, 1), None, A.bitwise_and))
+    V(ts(T.and1[:, 16:32], T.dmx[:, 16 * pb:16 * pb + 31:2], wanters(q ^ 2, 1), None, A.bitwise_and))
+    k = V(ts(T.and1[:, 32:40], T.dmx[:, 16 * o:16 * o + 15:2], wanters(q ^ 1, 0), None, A.bitwise_and))
+    V(ts(T.and1[:, 40:72], T.dmx[:, 0:63:2], 1 << (q ^ 4), None, A.bitwise_and))
+    vv(k)
+    k = V(ts(T.sel[:, 0:40], T.and1[:, 0:40], 0.0, None, A.is_gt))
+    kb = lift(T.lf1[:], T.sel[:, 0:16], k)
+    kc = V(ts(T.and1[:, 72:104], T.dmx[:, 0:63:2], 1 << q, None, A.bitwise_and))
+    vv(k)
+    need("v", "s", k_res)
+    k = V(scan(T.zz[:, 32:72], T.res[:, 0:40], T.sel[:, 0:40], 0.0, A.mult, A.add))
+    vv(kc)
+    kc = V(ts(T.sel[:, 40:104], T.and1[:, 40:104], 0.0, None, A.is_gt))
+    vv(k)
+    k = V(tp(T.x1t[:], T.zz[:, 40:72]))
+    need("v", "s", kb)
+    ka = V(tt_(T.ya1[:], T.zz[:, 32:48], T.lf1[:], A.add))
+    vv(k)
+    k = V(scan(T.zz[:, 105:136], T.ones[:, 0:31], T.x1t[:, 0:31], 0.0, A.mult, A.add))
+    vv(kc)
+    k_tt = V(tp(T.tt[:, 0:64], T.sel[:, 40:104]))
+    k_lf = lift(T.lf2[:], T.tt[:, 0:64], k_tt)
+    vv(k)
+    k_bs = V(tp(T.bs1[:], T.zz[:, 104:136]))
+    vv(ka)
+    ka = V(tt_(T.yc1[:], T.ya1[:], T.fj[:, 0:16], A.max))
+    vv(k_bs)
+    V(ts(T.sel[:, 104 + 8 * o:112 + 8 * o], T.zz[:, 64:72], T.bs1[:, 31:32], None, A.add))
+    k = V(ts(T.sel[:, 104 + 8 * pb:120 + 8 * pb], T.zz[:, 48:64], T.bs1[:, 23:24], 384.0, A.add, A.add))
+    vv(ka)
+    k_p1 = V(ts(T.p1[:], T.yc1[:].indirect(share1), T.bs1[:, 7:8], None, A.add))
+    vv(k)
+    k = V(cp(T.st1[:], T.sel[:, 104 + 8 * pa:120 + 8 * pa].indirect(share1)))
+    need("s", "v", k)
+    need("s", "s", k_rs)
+    k_vr1 = done("s", act(T.vr1[:], T.ramp[:].indirect(T.st1[:, 0:4]), CP))
+    kt = V(tp(T.tt[:, 64:96], T.sel[:, 104:136]))
+    kc = V(scan(T.inc2[:], T.res[:, 40:104], T.tt[:, 0:64], 0.0, A.mult, A.add))
+    vv(kt)
+    k = V(cp(T.st[:], T.tt[:, 64:96].indirect(share)))
+    need("v", "s", k_vr1)
+    k_w1 = V(cp(T.win1[:].indirect(T.p1[:, 0:4]), T.vr1[:]))
+    need("s", "v", k)
+    k_vr = done("s", act(T.vr2[:], T.ramp[:].indirect(T.st[:, 0:8]), CP))
+    k_f2 = done("s", act(T.win2[:, LB:LB + 256], T.zt[:, 0:256], ID, float(ZERO)))
+    vv(kc)
+    k_x2 = V(tp(T.x2t[:], T.inc2[:]))
+    vv(k_w1)
+    k_t1 = turn(1, 192)
+    need("v", "s", k_lf)
+    ka = V(tt_(T.ya2[:], T.inc2[:], T.lf2[:], A.add))
+    spread(1, 192, k_t1)
+    V(scan(T.zz[:, 137:168], T.ones[:, 0:31], T.x2t[:, 0:31], 0.0, A.mult, A.add))
+    k = V(scan(T.zz[:, 169:200], T.ones[:, 0:31], T.x2t[:, 32:63], 0.0, A.mult, A.add))
+    need("s", "v", k)
+    for c in range(2):
+        b = 32 * c
+        kn = done("s", act(T.tn[:, b:b + 32], T.ones[:], ID, T.x2t[:, b + 31:b + 32], T.zz[:, b + 167:b + 168]))
     if half == 0:
         k_fill = done("s", act(T.win3[:, LB:LB + 512], T.zt[:], ID, -1000.0))
     else:
         k_fill = done("s", act(T.win3[:, LB + 256:LB + 512], T.zt[:, 0:256], CP))
-    vv(k)
-    vv(V(scan(T.zz[:, 32:56], T.res[:, 0:24], T.sel[:, 0:24], 0.0, A.mult, A.add)))
-    k = V(tp(T.x1t[:], T.zz[:, 32:64]))
-    need("v", "s", kb)
-    ka = V(tt_(T.ya1[:], T.zz[:, 40:56], T.lf1[:], A.add))
-    vv(k)
-    k = V(scan(T.zz[:, 97:128], T.ones[:, 0:31], T.x1t[:, 0:31], 0.0, A.mult, A.add))
-    vv(ka)
-    ka = V(tt_(T.yc1[:], T.ya1[:], T.fj[:, 0:16], A.max))
-    vv(k)
-    vv(V(tp(T.bs1[:], T.zz[:, 96:128])))
-    k0 = V(ts(T.p0k[:], T.zz[:, 32:40], T.bs1[:, 7:8], None, A.add))
-    need("s", "v", k0)
-    need("s", "s", k_rs)
-    ks = done("s", act(T.v1r[:, o2:o2 + 128], T.ramp[:].indirect(T.p0k[:]), CP))
-    k_s2 = done("s", act(T.sel[:, 104 + 8 * o:112 + 8 * o], T.zz[:, 32:40], ID, T.bs1[:, 7:8]))
-    k_p1 = V(ts(T.p1[:], T.yc1[:], T.bs1[:, 23:24], None, A.add))
-    V(ts(T.and1[:, 40:72], T.dmx[:, 0:63:2], 1 << (q ^ 4), None, A.bitwise_and))
-    k = V(ts(T.and1[:, 72:104], T.dmx[:, 0:63:2], 1 << q, None, A.bitwise_and))
-    need("v", "gp", k_c2)
-    need("v", "s", k_sh)
-    k_ct = V(tp(T.ct[:, late], T.cst[:, late]))
-    vv(k)
-    V(ts(T.sel[:, 40:104], T.and1[:, 40:104], 0.0, None, A.is_gt))
-    vv(k_ct)
-    V(cp(T.gl[:, 2:12:2], T.ct[:, 96:256:32]))
-    need("v", "s", ks)
-    V(cp(T.win1[:].indirect(T.p1[:]), T.v1r[:]))
-    need("gp", "v", k_p1)
-    send(q ^ 2, T.p1r[:], T.p1[:], "rp")
-    copy(T.q2[:, 126:384], T.q0[:, 126:384], T.s2[:, 126:384], T.s0[:, 126:384], "cr", (("v", k_p1),))
+    copy(T.q2[:, 126:384], T.q0[:, 126:384], T.s2[:, 126:384], T.s0[:, 126:384], "cr")
     copy(T.q3[:, 256:258], T.q0[:, 126:128], T.s3[:, 256:258], T.s0[:, 126:128], "c3")
-    k_off1 = turn(1, 192)
+    vv(ka)
+    ka = V(tt_(T.yc2[:], T.ya2[:], T.fj[:], A.max))
+    vv(k)
+    k = V(tp(T.bs2[:], T.zz[:, 136:200]))
+    vv(k)
+    k_p2 = V(ts(T.p2[:], T.yc2[:, 0:32].indirect(share), T.bs2[:, 31:32], None, A.add))
+    if half == 0:
+        V(ts(T.p3[:], T.yc2[:, 32:64].indirect(share), T.bs2[:, 63:64], None, A.add))
+    vv(k_p2)
+    need("v", "s", k_f2)
+    k_w2 = V(cp(T.win2[:].indirect(T.p2[:, 0:8]), T.vr2[:]))
+    need("v", "s", kn)
+    k_n = V(tp(T.tnt[:], T.tn[:]))
+    nh = T.tnt[:, 63:64]
+    need("gp", "v", k_n)
+    send(q ^ 4, T.n2[:], T.tnt[:, 31:32], "rn")
+    vv(k_w2)
+    k_t2 = turn(2, 256)
+    if half == 0:
+        need("v", "s", k_ui)
+        vv(k_n)
+        V(ts(T.ub[:], T.ui[:], nh, 0.0, A.subtract, A.min))
+    spread(2, 256, k_t2)
+    copy(T.q2[:, 384:512], T.q1[:, 384:512], T.s2[:, 384:512], T.s1[:, 384:512], "cr", (("r0c", 16),), (("r0s", 16),))
+    copy(T.q3[:, 640:768], T.q1[:, 384:512], T.s3[:, 640:768], T.s1[:, 384:512], "c3")
+    merge(1, 192, T.m01[:, 16:28])
+    k_off1 = V(cp(T.off1[:], T.m01[:, 16:32].indirect(T.gl[:, 2:3])))
     ka, ks = pick(T.slq1[:], T.sls1[:], T.q1[:], T.s1[:], T.off1[:, 0:12], k_off1,
                   (("c1", 32), ("r0c", 16)), (("c1", 32), ("r0s", 16)))
     need("gp", "v", ka)
     send(q ^ 2, T.q2[:, 512:704].bitcast(dt.uint8), T.slq1[:].bitcast(dt.uint8), "r1c")
     need("gp", "s", ks)
     send(q ^ 2, T.s2[:, 512:704], T.sls1[:], "r1s")
-    copy(T.q2[:, 384:512], T.q1[:, 384:512], T.s2[:, 384:512], T.s1[:, 384:512], "cr",
-         (("v", ka), ("r0c", 16), ("r0s", 16)), (("s", ks),))
-    copy(T.q3[:, 640:768], T.q1[:, 384:512], T.s3[:, 640:768], T.s1[:, 384:512], "c3")
-
-    share = T.gl[:, 10:11]
-    need("v", "rp", 16)
-    vv(V(ts(T.sel[:, 104 + 8 * pb:120 + 8 * pb], T.p1r[:], float(385 - LB), 0.0, A.add, A.max)))
-    need("v", "s", k_s2)
-    k_tt = V(tp(T.tt[:], T.sel[:, 40:136]))
-    kb = lift(T.lf2[:], T.tt[:, 0:64], k_tt)
-    vv(k_tt)
-    ka = V(scan(T.inc2[:], T.res[:, 40:104], T.tt[:, 0:64], 0.0, A.mult, A.add))
-    k_st = V(cp(T.st[:], T.tt[:, 64:96].indirect(share)))
-    need("s", "v", k_st)
-    k_vr = done("s", act(T.vr2[:], T.ramp[:].indirect(T.st[:, 0:8]), CP))
-    vv(ka)
-    vv(V(tp(T.x2t[:], T.inc2[:])))
-    V(scan(T.zz[:, 129:160], T.ones[:, 0:31], T.x2t[:, 0:31], 0.0, A.mult, A.add))
-    k = V(scan(T.zz[:, 161:192], T.ones[:, 0:31], T.x2t[:, 32:63], 0.0, A.mult, A.add))
-    need("s", "v", k)
-    for c in range(2):
-        b = 32 * c
-        kn = done("s", act(T.tn[:, b:b + 32], T.ones[:], ID, T.x2t[:, b + 31:b + 32], T.zz[:, b + 159:b + 160]))
-    need("v", "s", kb)
-    ka = V(tt_(T.ya2[:], T.inc2[:], T.lf2[:], A.add))
-    vv(k)
-    V(tp(T.bs2[:], T.zz[:, 128:192]))
-    need("v", "s", kn)
-    k_n = V(tp(T.tnt[:], T.tn[:]))
-    nh = T.tnt[:, 63:64]
-    need("gp", "v", k_n)
-    send(q ^ 4, T.n2[:], T.tnt[:, 31:32], "rn")
-    vv(ka)
-    vv(V(tt_(T.yc2[:], T.ya2[:], T.fj[:], A.max)))
-    vv(V(ts(T.p2[:], T.yc2[:, 0:32].indirect(share), T.bs2[:, 31:32], None, A.add)))
-    need("v", "s", k_vr)
-    V(cp(T.win2[:].indirect(T.p2[:, 0:8]), T.vr2[:]))
-    spread(2, 256)
-    if half == 0:
-        k = V(ts(T.p3[:], T.yc2[:, 32:64].indirect(share), T.bs2[:, 63:64], None, A.add))
-    else:
+    if half:
         need("v", "rn", 16)
-        k = V(ts(T.p3[:], T.yc2[:, 32:64].indirect(share), T.bs2[:, 63:64], T.n2[:], A.add, A.add))
-    vv(k)
+        vv(V(ts(T.p3[:], T.yc2[:, 32:64].indirect(share), T.bs2[:, 63:64], T.n2[:], A.add, A.add)))
     need("v", "s", k_fill)
     need("v", "gp", k_gp3)
-    V(cp(T.win3[:].indirect(T.p3[:, 0:8]), T.vr2[:]))
-    spread(3, 512)
-    copy(T.q3[:, 768:960], T.q2[:, 512:704], T.s3[:, 768:960], T.s2[:, 512:704], "c3", (("r1c", 16), ("r1s", 16)))
-    merge(2, 256)
+    vv(V(cp(T.win3[:].indirect(T.p3[:, 0:8]), T.vr2[:])))
+    spread(3, 512, turn(3, 512))
+    copy(T.q3[:, 768:960], T.q2[:, 512:704], T.s3[:, 768:960], T.s2[:, 512:704], "c3", (("r1c", 16),), (("r1s", 16),))
+
+    def length_all():
+        need("v", "rn", 16)
+        V(ts(T.lnt[:, 0:1], nh, T.n2[:], None, A.add))
+
+    def length_own():
+        need("y", "v", V(red(T.lnt[:, 1:2], T.x2t[:, 32 + 8 * p4:40 + 8 * p4], X, A.add)))
+        g.sync.dma_start(T.ln[:], T.lnt[31:32, 0:2]).then_inc(S.lnd, 16)
+
+    merge(2, 256, T.m2[:], (length_all, length_own))
     k_off2 = V(cp(T.off2[:], T.m2[:].indirect(T.gl[:, 4:5])))
     ka, ks = pick(T.slq2[:], T.sls2[:], T.q2[:], T.s2[:], T.off2[:], k_off2, (("cr", 64), ("r1c", 16)), (("cr", 64), ("r1s", 16)))
     need("gp", "v", ka)
@@ -342,71 +384,59 @@ def rank_program(g, core, T, topo):
     need("gp", "s", ks)
     send(q ^ 4, T.s3[:, 0:256], T.sls2[:], "r2s")
 
-    V(g.vector.quantize_mx(T.q3[:, 384:640], T.s3[:, 384:640], T.xt[:, 8:1032]))
-    need("v", "lw", 16)
-    k_wq = V(g.vector.quantize_mx(T.wq[:], T.ws[:], T.wt[:]))
+    k_wq = []
+
+    def quant_w():
+        need("v", "lw", 16)
+        k_wq.append(V(g.vector.quantize_mx(T.wq[:], T.ws[:], T.wt[:])))
+
+    def quant_x():
+        V(g.vector.quantize_mx(T.q3[:, 384:640], T.s3[:, 384:640], T.xt[:, 8:1032]))
+
+    merge(3, 512, T.m3[:], (quant_x, quant_w))
+    lo3, hi3 = T.m3[:, 0:24].indirect(T.gl[:, 6:7]), T.m3[:, 8:32].indirect(T.gl[:, 6:7])
     if half == 0:
-        need("s", "gp", k_gp3)
-        need("s", "v", k_ct)
-        ku = done("s", act(T.ui[:], T.uif[:], ID, T.ct[:, 256:257]))
-        need("v", "s", ku)
-        V(ts(T.ub[:], T.ui[:], nh, 0.0, A.subtract, A.min))
-    merge(3, 512)
-    if half == 0:
-        for c in range(2):
-            k = V(tt_(T.tm[:, 16 * c:16 * c + 16], T.m3[:].indirect(T.gl[:, 6 + 2 * c:7 + 2 * c]), T.ub[:, 16 * c:16 * c + 16], A.max))
-        vv(k)
+        V(tt_(T.tm[:, 0:16], lo3, T.ub[:, 0:16], A.max))
+        vv(V(tt_(T.tm[:, 16:32], hi3, T.ub[:, 16:32], A.max)))
         k_off3 = V(ts(T.off3[:], T.tm[:], 256.0, None, A.add))
     else:
-        V(cp(T.off3[:, 16:32], T.m3[:].indirect(T.gl[:, 8:9])))
-        k_off3 = V(ts(T.off3[:, 0:16], T.m3[:].indirect(T.gl[:, 6:7]), 256.0, None, A.add))
+        V(cp(T.off3[:, 16:32], hi3))
+        k_off3 = V(ts(T.off3[:, 0:16], lo3, 256.0, None, A.add))
 
-    def product(c, lo, vwaits, swaits):
-        a, b = 256 * c, 256 * c + 256
-        ka, kb = pick(T.qa[:, a:b], T.sa[:, a:b], T.q3[:, lo:960], T.s3[:, lo:960], T.off3[:, 16 * c:16 * c + 16], k_off3,
+    def product(i, a, b, lo, vwaits, swaits):
+        w_ = b - a
+        ka, kb = pick(T.qa[:, a:b], T.sa[:, a:b], T.q3[:, lo:960], T.s3[:, lo:960], T.off3[:, a // 16:b // 16], k_off3,
                       vwaits, swaits)
         need("t", "v", ka)
         need("t", "s", kb)
         for w in range(2):
-            done("t", g.tensor.matmul_mx(T.ps[:, 512 * (2 * w + c):512 * (2 * w + c) + 256], T.wq[:, 128 * w:128 * w + 128],
+            e = 512 * (2 * i + w)
+            done("t", g.tensor.matmul_mx(T.ps[:, e:e + w_], T.wq[:, 128 * w:128 * w + 128],
                                          T.ws[:, 128 * w:128 * w + 128], T.qa[:, a:b], T.sa[:, a:b], True, True))
         return n["t"]
 
-    def store(c, k):
+    def store(a, b, i, k):
+        e, w_ = 1024 * i, b - a
         need("v", "t", k - 1)
         need("s", "t", k)
-        a = V(cp(T.ys[:, 256 * c:256 * c + 256], T.ps[:, 512 * c:512 * c + 256]))
-        b = done("s", act(T.ys[:, 512 + 256 * c:768 + 256 * c], T.ps[:, 1024 + 512 * c:1280 + 512 * c], CP))
-        need("y", "v", a)
-        g.sync.dma_start(T.y[:, 256 * c:256 * c + 256], T.ys[:, 256 * c:256 * c + 256]).then_inc(S.yo, 16)
-        need("y", "s", b)
-        g.sync.dma_start(T.y[:, 512 + 256 * c:768 + 256 * c], T.ys[:, 512 + 256 * c:768 + 256 * c]).then_inc(S.yo, 16)
+        ka = V(cp(T.ys[:, a:b], T.ps[:, e:e + w_]))
+        kb = done("s", act(T.ys[:, 512 + a:512 + b], T.ps[:, e + 512:e + 512 + w_], CP))
+        need("y", "v", ka)
+        g.sync.dma_start(T.y[:, a:b], T.ys[:, a:b]).then_inc(S.yo, 16)
+        need("y", "s", kb)
+        g.sync.dma_start(T.y[:, 512 + a:512 + b], T.ys[:, 512 + a:512 + b]).then_inc(S.yo, 16)
+        n_yo[0] += 32
 
-    def lengths():
-        need("v", "rn", 16)
-        V(ts(T.lnt[:, 0:1], nh, T.n2[:], None, A.add))
-        return V(red(T.lnt[:, 1:2], T.x2t[:, 32 + 8 * p4:40 + 8 * p4], X, A.add))
-
-    need("t", "v", k_wq)
+    need("t", "v", k_wq[0])
     held, r2 = ("c3", 96), (("r2c", 16), ("r2s", 16))
-    if half == 0:
-        k0 = product(0, 0, (held, r2[0]), (held, r2[1]))
-        k1 = product(1, 0, (), ())
-        store(0, k0)
-        k_ln = lengths()
-        store(1, k1)
-    else:
-        k1 = product(1, 256, (held,), (held,))
-        k0 = product(0, 0, (r2[0],), (r2[1],))
-        store(1, k1)
-        k_ln = lengths()
-        store(0, k0)
-    need("y", "v", k_ln)
-    g.sync.dma_start(T.ln[:], T.lnt[31:32, 0:2]).then_inc(S.lnd, 16)
+    runs = [(0, 128, 0), (128, 384, 0), (384, 512, 0)] if half == 0 else [(256, 512, 256), (0, 128, 0), (128, 256, 0)]
+    ends = [product(i, a, b, lo, [held] + [r2[0]] * (lo == 0), [held] + [r2[1]] * (lo == 0)) for i, (a, b, lo) in enumerate(runs)]
+    for i, (a, b, lo) in enumerate(runs):
+        store(a, b, i, ends[i])
 
     for kind in ("v", "s", "t"):
         need("gp", kind, n[kind])
     g.wait_ge(S.gp, n["gp"])
     g.wait_ge(S.lo, n_lo[0])
-    g.wait_ge(S.yo, 64)
+    g.wait_ge(S.yo, n_yo[0])
     g.wait_ge(S.lnd, 16)

from concourse.bass import DstId, RemoteDMATransfer
from concourse.mybir import dt, AluOpType, AxisListType, ActivationFunctionType

F32, I32, BF, U16, U8, Q8 = "float32", "int32", "bfloat16", "uint16", "uint8", "float8_e4m3fn_x4"
LB = 4864
ZERO = 127


def _s(n, d):
    return ("sbuf", [128, n], d)


SCRATCH = {
    "dmx": _s(64, I32), "xt": _s(1032, BF), "wt": _s(1024, BF), "zt": _s(512, BF),
    "q0": _s(384, Q8), "s0": _s(384, U8), "q1": _s(512, Q8), "s1": _s(512, U8),
    "q2": _s(704, Q8), "s2": _s(704, U8), "q3": _s(960, Q8), "s3": _s(960, U8),
    "slq0": _s(128, Q8), "sls0": _s(128, U8), "slq1": _s(192, Q8), "sls1": _s(192, U8),
    "slq2": _s(256, Q8), "sls2": _s(256, U8),
    "qa": _s(512, Q8), "sa": _s(512, U8), "wq": _s(256, Q8), "ws": _s(256, U8),
    "pa": _s(1, I32), "pb": _s(1, I32), "bi": _s(8, I32), "bf": _s(8, F32), "c5": _s(1, F32),
    "gl": _s(12, U16), "ones": _s(32, F32), "c8": _s(8, F32),
    "fj": _s(64, F32), "vraw": _s(128, F32), "v1r": _s(128, F32),
    "ramp": _s(577, F32), "res": _s(104, F32), "uif": _s(32, F32), "ui": _s(32, F32), "ub": _s(32, F32),
    "zz": _s(200, F32), "and0": _s(8, I32), "sel0": _s(8, F32), "lf0": _s(8, F32), "x0t": _s(32, F32), "bs0": _s(32, F32),
    "ya0": _s(8, F32), "yc0": _s(8, F32), "p0": _s(8, U16),
    "and1": _s(104, I32), "sel": _s(136, F32), "lf1": _s(16, F32), "x1t": _s(32, F32), "bs1": _s(32, F32),
    "ya1": _s(16, F32), "yc1": _s(16, F32), "p1": _s(16, U16), "st1": _s(16, U16), "vr1": _s(64, F32),
    "tt": _s(96, F32), "st": _s(16, U16), "vr2": _s(128, F32), "lf2": _s(64, F32), "inc2": _s(64, F32), "x2t": _s(64, F32),
    "bs2": _s(64, F32), "tn": _s(64, F32), "tnt": _s(64, F32), "n2": _s(1, F32),
    "ya2": _s(64, F32), "yc2": _s(64, F32), "p2": _s(16, U16), "p3": _s(16, U16),
    "win0": _s(LB + 144, F32), "win1": _s(LB + 192, F32), "win2": _s(LB + 256, F32), "win3": _s(LB + 512, F32),
    "tr0": _s(288, F32), "tr1": _s(192, F32), "tr2": _s(256, F32), "tr3": _s(512, F32),
    "m01": _s(32, F32), "z1": _s(48, F32), "h1": _s(24, F32), "z2": _s(64, F32), "h2": _s(32, F32), "m2": _s(16, F32),
    "z3": _s(128, F32), "h3": _s(64, F32), "m3": _s(32, F32), "tm": _s(32, F32),
    "off0": _s(16, U16), "off1": _s(16, U16), "off2": _s(16, U16), "off3": _s(32, U16),
    "lnt": _s(4, F32), "ys": _s(1024, F32),
    "ps": ("psum", [128, 4096], F32),
}
SEMAPHORES = ["ld", "lx", "lw", "v", "s", "t", "gp", "mk", "r0c", "r0s", "r1c", "r1s", "r2c", "r2s", "rn",
              "c1", "cr", "c3", "d1", "d2", "d3", "lo", "yo", "lnd"]


def wanters(q, b):
    return sum(1 << e for e in range(8) if (e ^ q ^ (1 << b)) % (2 << b) == 0)


def rank_program(g, core, T, topo):
    q = T.rank_of(core)
    if q is None:
        return
    A, X = AluOpType, AxisListType.X
    CP, ID = ActivationFunctionType.Copy, ActivationFunctionType.Identity
    S = T.sem
    p4, half = q & 3, q >> 2
    own = slice(16 * p4, 16 * p4 + 15)
    queues = {"v": g.vector, "s": g.scalar, "t": g.tensor, "gp": g, "y": g.sync}
    n, seen, n_lo, n_yo = {"v": 0, "s": 0, "t": 0, "gp": 0}, {}, [0], [0]

    def need(queue, sem, count):
        if seen.get((queue, sem), 0) < count:
            queues[queue].wait_ge(S[sem], int(count))
            seen[(queue, sem)] = count

    def done(kind, ins):
        ins.then_inc(S[kind], 1)
        n[kind] += 1
        return n[kind]

    def V(ins):
        return done("v", ins)

    def vv(count=None):
        need("v", "v", n["v"] if count is None else count)

    ts, tt_, cp = g.vector.tensor_scalar, g.vector.tensor_tensor, g.vector.tensor_copy
    red, tp, scan = g.vector.tensor_reduce, g.vector.transpose, g.vector.tensor_tensor_scan
    act = g.scalar.activation

    def to(d):
        return T.cores[d]

    def send(dst, out, in_, sem):
        rid, pid, _ = topo.addr(to(dst))
        g.remote_dma(out, in_, S[sem], S.lo, pid, rid, topo.mask(core, to(dst)))
        n_lo[0] += len(topo.engines(core, to(dst)))

    def copy(out_q, in_q, out_s, in_s, sem, wq=(), ws=()):
        for w in wq:
            need("y", *w)
        g.sync.dma_start(out_q.bitcast(dt.uint8), in_q.bitcast(dt.uint8)).then_inc(S[sem], 16)
        for w in ws:
            need("y", *w)
        g.sync.dma_start(out_s, in_s).then_inc(S[sem], 16)

    for a in range(4):
        for h in range(2):
            e = g.sync if h == 0 else g.scalar
            e.dma_start(T.dmx[32 * a + 16 * h:32 * a + 16 * h + 16, own], T.dm[:, h:h + 15]).then_inc(S.ld, 16)
    g.sync.dma_start(T.xt[:, 8:1032], T.x[:]).then_inc(S.lx, 16)

    def iota(out, pat, base, cm=0):
        return done("gp", g.iota(out, pat, base, cm, allow_small_or_imprecise_dtypes=True))

    k_pa = done("gp", g.iota(T.pa[:], [[0, 1]], 0, 129))
    k_pb = done("gp", g.iota(T.pb[:], [[0, 1]], 0, 17))
    k_vraw = iota(T.vraw[:], [[32, 8], [1, 16]], 128)
    k_fj = iota(T.fj[:], [[0, 2], [1, 32]], 0, 32)

    k_zt = V(g.vector.memset(T.zt[:, 0:208], 0.0))
    need("s", "v", k_zt)
    done("s", act(T.ones[:], T.zt[:, 0:32], ID, 1.0))
    k_zz = done("s", act(T.zz[:], T.zt[:, 0:200], CP))
    done("s", act(T.win0[:, LB - 16:LB + 144], T.zt[:, 0:160], ID, 128.0))
    k_m0 = done("s", act(T.m01[:], T.zt[:, 0:32], CP))

    def bits(c, src, shift, mask):
        need("v", "gp", k_pb if c == 1 else k_pa)
        if shift:
            return V(ts(T.bi[:, c:c + 1], src[:], shift, mask, A.logical_shift_right, A.bitwise_and))
        return V(ts(T.bi[:, c:c + 1], src[:], mask, None, A.bitwise_and))

    bits(0, T.pa, 0, 16)
    bits(2, T.pa, 1, 7)
    bits(3, T.pa, 0, 31)
    bits(4, T.pa, 0, 15)
    k_bi = bits(1, T.pb, 4, 1)
    V(g.vector.memset(T.xt[:, 0:8], 0.0))
    vv(k_bi)
    k_bf = V(cp(T.bf[:, 0:5], T.bi[:, 0:5]))
    ei = T.bf[:, 2:3]

    peers = [q ^ 1, q ^ 2, q ^ 3]
    g.wait_ge(S.ld, 128)
    m = topo.mask(core, to(peers[0]))
    ids = []
    for d in peers:
        m &= topo.mask(core, to(d))
        rid, pid, _ = topo.addr(to(d))
        ids.append(DstId(rid=rid, pnc=pid))
    g.remote_dma_fused([RemoteDMATransfer(dst_ids=ids, dma_engine_mask=m, remote_sem=S.mk, srcs=[T.dmx[:, own]],
                                          dsts=[T.dmx[:, own] for d in peers])], local_sem=S.lo)
    n_lo[0] += bin(m).count("1")
    k_c8 = iota(T.c8[:], [[32, 8]], 129)
    k_ramp = iota(T.ramp[:, 129:385], [[1, 256]], 128)
    if half == 0:
        k_gp3 = iota(T.uif[:], [[16, 32]], -256)
    else:
        k_gp3 = iota(T.win3[:, LB:LB + 256], [[1, 256]], -256)

    def turn(i, count):
        return V(tp(T["tr%d" % i][:], T["win%d" % i][:, LB:LB + count]))

    def spread(i, count, k):
        tr, z, nb, sem = T["tr%d" % i], T["z%d" % i], count // 32, "d%d" % i
        vv(k)
        k = V(tt_(z[:, 0:nb], tr[:, 0:count:32], tr[:, 16:count:32], A.max))
        need("y", "v", k)
        need("s", "v", k)
        for s in range(1, 8):
            c, a = slice(nb * s, nb * s + nb), 16 * s
            g.sync.dma_start(z[0:128 - a, c], z[a:128, 0:nb]).then_inc(S[sem], 16)
            g.scalar.dma_start(z[128 - a:128, c], z[0:a, 0:nb]).then_inc(S[sem], 16)

    def merge(i, count, out, fill=()):
        z, h, nb = T["z%d" % i], T["h%d" % i], count // 32
        need("v", "d%d" % i, 224)
        k = V(tt_(h[:], z[:, 0:4 * nb], z[:, 4 * nb:8 * nb], A.max))
        if fill:
            fill[0]()
        vv(k)
        k = V(tt_(out, h[:, 0:2 * nb], h[:, 2 * nb:4 * nb], A.max))
        if fill:
            fill[1]()
        vv(k)

    def pick(qo, so, qi, si, off, k_off, vwaits=(), swaits=()):
        vv(k_off)
        for w in vwaits:
            need("v", *w)
        a = V(cp(qo.bitcast(dt.uint32), qi.bitcast(dt.uint32).indirect(off)))
        need("s", "v", k_off)
        for w in swaits:
            need("s", *w)
        return a, done("s", act(so, si.indirect(off), CP))

    def lift(out, sel, k):
        need("s", "v", k)
        return done("s", act(out, sel, CP, 0.0, float(LB - 1)))

    def last_gather(c, nb):
        return V(ts(T.gl[:, c:c + 1], T.bf[:, 1:2], nb, ei, A.mult, A.add))

    need("v", "ld", 128)
    k = V(ts(T.and0[:], T.dmx[:, 16 * p4:16 * p4 + 15:2], wanters(q, 0), None, A.bitwise_and))
    bits(5, T.pa, 5, 15)
    vv(k)
    k = V(ts(T.sel0[:], T.and0[:], 0.0, None, A.is_gt))
    kb = lift(T.lf0[:], T.sel0[:], k)
    k_bi = bits(6, T.pa, 5, 31)
    need("s", "v", k_bf)
    need("s", "gp", k_vraw)
    k_v1 = done("s", act(T.v1r[:], T.vraw[:], ID, T.bf[:, 0:1]))
    k1 = done("s", act(T.res[:], T.zt[:, 0:104], ID, 1.0))
    vv(k)
    need("v", "s", k_zz)
    k = V(scan(T.zz[:, 0:8], T.ones[:, 0:8], T.sel0[:], 0.0, A.mult, A.add))
    vv(k_bf)
    k_c5 = V(ts(T.c5[:], T.bf[:, 0:1], -0.0625, 5.0, A.mult, A.add))
    vv(k)
    k = V(tp(T.x0t[:], T.zz[:, 0:32]))
    need("v", "s", kb)
    ka = V(tt_(T.ya0[:], T.zz[:, 0:8], T.lf0[:], A.add))
    vv(k)
    k = V(scan(T.zz[:, 73:104], T.ones[:, 0:31], T.x0t[:, 0:31], 0.0, A.mult, A.add))
    vv(ka)
    need("v", "gp", k_fj)
    V(tt_(T.yc0[:], T.ya0[:], T.fj[:, 0:8], A.max))
    vv(k)
    k = V(tp(T.bs0[:], T.zz[:, 72:104]))
    V(cp(T.gl[:, 8:12:2], T.bi[:, 5:7]))
    vv(k)
    k = V(ts(T.p0[:], T.yc0[:], T.bs0[:, 7:8], None, A.add))
    V(ts(T.gl[:, 0:1], T.bf[:, 1:2], T.c5[:], ei, A.mult, A.add))
    need("y", "v", k)
    g.sync.dma_start(T.wt[:], T.w[:]).then_inc(S.lw, 16)
    vv(k)
    need("v", "s", k_v1)
    k_w0 = V(cp(T.win0[:].indirect(T.p0[:]), T.v1r[:]))
    need("v", "lx", 16)
    V(g.vector.quantize_mx(T.q0[:, 126:384], T.s0[:, 126:384], T.xt[:]))
    need("s", "s", k1)
    done("s", act(T.res[:, 16:33:16], T.zt[:, 0:2], CP))
    done("s", act(T.res[:, 72:73], T.zt[:, 0:1], CP))
    need("s", "gp", k_c8)
    k_res = done("s", act(T.sel[:, 104 + 8 * p4:112 + 8 * p4], T.c8[:], ID, T.bf[:, 3:4]))
    need("s", "gp", k_ramp)
    done("s", act(T.ramp[:, 0:129], T.ramp[:, 129:258], ID, 255.0))
    k_rs = done("s", act(T.ramp[:, 385:577], T.ramp[:, 129:321], ID, 384.0))
    k_ui = done("s", act(T.win1[:, LB:LB + 192], T.zt[:, 0:192], ID, 128.0))
    if half == 0:
        need("s", "gp", k_gp3)
        k_ui = done("s", act(T.ui[:], T.uif[:], ID, T.bf[:, 4:5]))
    vv(k_w0)
    V(tp(T.tr0[:, 0:128], T.win0[:, LB:LB + 128]))
    k0 = V(tp(T.tr0[:, 128:288], T.win0[:, LB - 16:LB + 144]))
    last_gather(2, 6.0)
    last_gather(4, 8.0)
    vv(k0)
    need("v", "s", k_m0)
    k0 = V(tt_(T.m01[:, 0:9], T.tr0[:, 0:288:32], T.tr0[:, 16:288:32], A.max))
    last_gather(6, 16.0)
    vv(k0)
    k0 = V(cp(T.off0[:], T.m01[:, 0:16].indirect(T.gl[:, 0:1])))
    V(g.vector.memset(T.zt[:, 208:512], 0.0))
    k0, ks = pick(T.slq0[:], T.sls0[:], T.q0[:], T.s0[:], T.off0[:, 0:8], k0)
    need("gp", "v", k0)
    send(q ^ 1, T.q1[:, 384:512].bitcast(dt.uint8), T.slq0[:].bitcast(dt.uint8), "r0c")
    need("gp", "s", ks)
    send(q ^ 1, T.s1[:, 384:512], T.sls0[:], "r0s")
    copy(T.q1[:, 128:384], T.q0[:, 128:384], T.s1[:, 128:384], T.s0[:, 128:384], "c1", (("v", k0),), (("s", ks),))

    pa, pb, o = 2 * (p4 >> 1), 2 * (1 - (p4 >> 1)), p4 ^ 1
    share1, share = T.gl[:, 8:9], T.gl[:, 10:11]
    need("v", "mk", 48)
    V(ts(T.and1[:, 0:16], T.dmx[:, 16 * pa:16 * pa + 31:2], wanters(q, 1), None, A.bitwise_and))
    V(ts(T.and1[:, 16:32], T.dmx[:, 16 * pb:16 * pb + 31:2], wanters(q ^ 2, 1), None, A.bitwise_and))
    k = V(ts(T.and1[:, 32:40], T.dmx[:, 16 * o:16 * o + 15:2], wanters(q ^ 1, 0), None, A.bitwise_and))
    V(ts(T.and1[:, 40:72], T.dmx[:, 0:63:2], 1 << (q ^ 4), None, A.bitwise_and))
    vv(k)
    k = V(ts(T.sel[:, 0:40], T.and1[:, 0:40], 0.0, None, A.is_gt))
    kb = lift(T.lf1[:], T.sel[:, 0:16], k)
    kc = V(ts(T.and1[:, 72:104], T.dmx[:, 0:63:2], 1 << q, None, A.bitwise_and))
    vv(k)
    need("v", "s", k_res)
    k = V(scan(T.zz[:, 32:72], T.res[:, 0:40], T.sel[:, 0:40], 0.0, A.mult, A.add))
    vv(kc)
    kc = V(ts(T.sel[:, 40:104], T.and1[:, 40:104], 0.0, None, A.is_gt))
    vv(k)
    k = V(tp(T.x1t[:], T.zz[:, 40:72]))
    need("v", "s", kb)
    ka = V(tt_(T.ya1[:], T.zz[:, 32:48], T.lf1[:], A.add))
    vv(k)
    k = V(scan(T.zz[:, 105:136], T.ones[:, 0:31], T.x1t[:, 0:31], 0.0, A.mult, A.add))
    vv(kc)
    k_tt = V(tp(T.tt[:, 0:64], T.sel[:, 40:104]))
    k_lf = lift(T.lf2[:], T.tt[:, 0:64], k_tt)
    vv(k)
    k_bs = V(tp(T.bs1[:], T.zz[:, 104:136]))
    vv(ka)
    ka = V(tt_(T.yc1[:], T.ya1[:], T.fj[:, 0:16], A.max))
    vv(k_bs)
    V(ts(T.sel[:, 104 + 8 * o:112 + 8 * o], T.zz[:, 64:72], T.bs1[:, 31:32], None, A.add))
    k = V(ts(T.sel[:, 104 + 8 * pb:120 + 8 * pb], T.zz[:, 48:64], T.bs1[:, 23:24], 384.0, A.add, A.add))
    vv(ka)
    k_p1 = V(ts(T.p1[:], T.yc1[:].indirect(share1), T.bs1[:, 7:8], None, A.add))
    vv(k)
    k = V(cp(T.st1[:], T.sel[:, 104 + 8 * pa:120 + 8 * pa].indirect(share1)))
    need("s", "v", k)
    need("s", "s", k_rs)
    k_vr1 = done("s", act(T.vr1[:], T.ramp[:].indirect(T.st1[:, 0:4]), CP))
    kt = V(tp(T.tt[:, 64:96], T.sel[:, 104:136]))
    kc = V(scan(T.inc2[:], T.res[:, 40:104], T.tt[:, 0:64], 0.0, A.mult, A.add))
    vv(kt)
    k = V(cp(T.st[:], T.tt[:, 64:96].indirect(share)))
    need("v", "s", k_vr1)
    k_w1 = V(cp(T.win1[:].indirect(T.p1[:, 0:4]), T.vr1[:]))
    need("s", "v", k)
    k_vr = done("s", act(T.vr2[:], T.ramp[:].indirect(T.st[:, 0:8]), CP))
    k_f2 = done("s", act(T.win2[:, LB:LB + 256], T.zt[:, 0:256], ID, float(ZERO)))
    vv(kc)
    k_x2 = V(tp(T.x2t[:], T.inc2[:]))
    vv(k_w1)
    k_t1 = turn(1, 192)
    need("v", "s", k_lf)
    ka = V(tt_(T.ya2[:], T.inc2[:], T.lf2[:], A.add))
    spread(1, 192, k_t1)
    V(scan(T.zz[:, 137:168], T.ones[:, 0:31], T.x2t[:, 0:31], 0.0, A.mult, A.add))
    k = V(scan(T.zz[:, 169:200], T.ones[:, 0:31], T.x2t[:, 32:63], 0.0, A.mult, A.add))
    need("s", "v", k)
    for c in range(2):
        b = 32 * c
        kn = done("s", act(T.tn[:, b:b + 32], T.ones[:], ID, T.x2t[:, b + 31:b + 32], T.zz[:, b + 167:b + 168]))
    if half == 0:
        k_fill = done("s", act(T.win3[:, LB:LB + 512], T.zt[:], ID, -1000.0))
    else:
        k_fill = done("s", act(T.win3[:, LB + 256:LB + 512], T.zt[:, 0:256], CP))
    copy(T.q2[:, 126:384], T.q0[:, 126:384], T.s2[:, 126:384], T.s0[:, 126:384], "cr")
    copy(T.q3[:, 256:258], T.q0[:, 126:128], T.s3[:, 256:258], T.s0[:, 126:128], "c3")
    vv(ka)
    ka = V(tt_(T.yc2[:], T.ya2[:], T.fj[:], A.max))
    vv(k)
    k = V(tp(T.bs2[:], T.zz[:, 136:200]))
    vv(k)
    k_p2 = V(ts(T.p2[:], T.yc2[:, 0:32].indirect(share), T.bs2[:, 31:32], None, A.add))
    if half == 0:
        V(ts(T.p3[:], T.yc2[:, 32:64].indirect(share), T.bs2[:, 63:64], None, A.add))
    vv(k_p2)
    need("v", "s", k_f2)
    k_w2 = V(cp(T.win2[:].indirect(T.p2[:, 0:8]), T.vr2[:]))
    need("v", "s", kn)
    k_n = V(tp(T.tnt[:], T.tn[:]))
    nh = T.tnt[:, 63:64]
    need("gp", "v", k_n)
    send(q ^ 4, T.n2[:], T.tnt[:, 31:32], "rn")
    vv(k_w2)
    k_t2 = turn(2, 256)
    if half == 0:
        need("v", "s", k_ui)
        vv(k_n)
        V(ts(T.ub[:], T.ui[:], nh, 0.0, A.subtract, A.min))
    spread(2, 256, k_t2)
    copy(T.q2[:, 384:512], T.q1[:, 384:512], T.s2[:, 384:512], T.s1[:, 384:512], "cr", (("r0c", 16),), (("r0s", 16),))
    copy(T.q3[:, 640:768], T.q1[:, 384:512], T.s3[:, 640:768], T.s1[:, 384:512], "c3")
    merge(1, 192, T.m01[:, 16:28])
    k_off1 = V(cp(T.off1[:], T.m01[:, 16:32].indirect(T.gl[:, 2:3])))
    ka, ks = pick(T.slq1[:], T.sls1[:], T.q1[:], T.s1[:], T.off1[:, 0:12], k_off1,
                  (("c1", 32), ("r0c", 16)), (("c1", 32), ("r0s", 16)))
    need("gp", "v", ka)
    send(q ^ 2, T.q2[:, 512:704].bitcast(dt.uint8), T.slq1[:].bitcast(dt.uint8), "r1c")
    need("gp", "s", ks)
    send(q ^ 2, T.s2[:, 512:704], T.sls1[:], "r1s")
    if half:
        need("v", "rn", 16)
        vv(V(ts(T.p3[:], T.yc2[:, 32:64].indirect(share), T.bs2[:, 63:64], T.n2[:], A.add, A.add)))
    need("v", "s", k_fill)
    need("v", "gp", k_gp3)
    vv(V(cp(T.win3[:].indirect(T.p3[:, 0:8]), T.vr2[:])))
    spread(3, 512, turn(3, 512))
    copy(T.q3[:, 768:960], T.q2[:, 512:704], T.s3[:, 768:960], T.s2[:, 512:704], "c3", (("r1c", 16),), (("r1s", 16),))

    def length_all():
        need("v", "rn", 16)
        V(ts(T.lnt[:, 0:1], nh, T.n2[:], None, A.add))

    def length_own():
        need("y", "v", V(red(T.lnt[:, 1:2], T.x2t[:, 32 + 8 * p4:40 + 8 * p4], X, A.add)))
        g.sync.dma_start(T.ln[:], T.lnt[31:32, 0:2]).then_inc(S.lnd, 16)

    merge(2, 256, T.m2[:], (length_all, length_own))
    k_off2 = V(cp(T.off2[:], T.m2[:].indirect(T.gl[:, 4:5])))
    ka, ks = pick(T.slq2[:], T.sls2[:], T.q2[:], T.s2[:], T.off2[:], k_off2, (("cr", 64), ("r1c", 16)), (("cr", 64), ("r1s", 16)))
    need("gp", "v", ka)
    send(q ^ 4, T.q3[:, 0:256].bitcast(dt.uint8), T.slq2[:].bitcast(dt.uint8), "r2c")
    need("gp", "s", ks)
    send(q ^ 4, T.s3[:, 0:256], T.sls2[:], "r2s")

    k_wq = []

    def quant_w():
        need("v", "lw", 16)
        k_wq.append(V(g.vector.quantize_mx(T.wq[:], T.ws[:], T.wt[:])))

    def quant_x():
        V(g.vector.quantize_mx(T.q3[:, 384:640], T.s3[:, 384:640], T.xt[:, 8:1032]))

    merge(3, 512, T.m3[:], (quant_x, quant_w))
    lo3, hi3 = T.m3[:, 0:24].indirect(T.gl[:, 6:7]), T.m3[:, 8:32].indirect(T.gl[:, 6:7])
    if half == 0:
        V(tt_(T.tm[:, 0:16], lo3, T.ub[:, 0:16], A.max))
        vv(V(tt_(T.tm[:, 16:32], hi3, T.ub[:, 16:32], A.max)))
        k_off3 = V(ts(T.off3[:], T.tm[:], 256.0, None, A.add))
    else:
        V(cp(T.off3[:, 16:32], hi3))
        k_off3 = V(ts(T.off3[:, 0:16], lo3, 256.0, None, A.add))

    def product(i, a, b, lo, vwaits, swaits):
        w_ = b - a
        ka, kb = pick(T.qa[:, a:b], T.sa[:, a:b], T.q3[:, lo:960], T.s3[:, lo:960], T.off3[:, a // 16:b // 16], k_off3,
                      vwaits, swaits)
        need("t", "v", ka)
        need("t", "s", kb)
        for w in range(2):
            e = 512 * (2 * i + w)
            done("t", g.tensor.matmul_mx(T.ps[:, e:e + w_], T.wq[:, 128 * w:128 * w + 128],
                                         T.ws[:, 128 * w:128 * w + 128], T.qa[:, a:b], T.sa[:, a:b], True, True))
        return n["t"]

    def store(a, b, i, k):
        e, w_ = 1024 * i, b - a
        need("v", "t", k - 1)
        need("s", "t", k)
        ka = V(cp(T.ys[:, a:b], T.ps[:, e:e + w_]))
        kb = done("s", act(T.ys[:, 512 + a:512 + b], T.ps[:, e + 512:e + 512 + w_], CP))
        need("y", "v", ka)
        g.sync.dma_start(T.y[:, a:b], T.ys[:, a:b]).then_inc(S.yo, 16)
        need("y", "s", kb)
        g.sync.dma_start(T.y[:, 512 + a:512 + b], T.ys[:, 512 + a:512 + b]).then_inc(S.yo, 16)
        n_yo[0] += 32

    need("t", "v", k_wq[0])
    held, r2 = ("c3", 96), (("r2c", 16), ("r2s", 16))
    runs = [(0, 128, 0), (128, 384, 0), (384, 512, 0)] if half == 0 else [(256, 512, 256), (0, 128, 0), (128, 256, 0)]
    ends = [product(i, a, b, lo, [held] + [r2[0]] * (lo == 0), [held] + [r2[1]] * (lo == 0)) for i, (a, b, lo) in enumerate(runs)]
    for i, (a, b, lo) in enumerate(runs):
        store(a, b, i, ends[i])

    for kind in ("v", "s", "t"):
        need("gp", kind, n[kind])
    g.wait_ge(S.gp, n["gp"])
    g.wait_ge(S.lo, n_lo[0])
    g.wait_ge(S.yo, n_yo[0])
    g.wait_ge(S.lnd, 16)
